import numpy as np
import ml_dtypes


def mxq(x, axis, fmt="e4m3"):
    dtype, down = {"e4m3": (ml_dtypes.float8_e4m3fn, 7), "e5m2": (ml_dtypes.float8_e5m2, 14)}[fmt]
    v = np.moveaxis(np.asarray(x, np.float32).astype(ml_dtypes.bfloat16).astype(np.float64), axis, -1)
    blocks = v.reshape(v.shape[:-1] + (-1, 32))
    amax = np.abs(blocks).max(-1, keepdims=True)
    byte = np.maximum(np.where(amax > 0, np.frexp(amax)[1] - 1 + 127, 0) - down, 1)
    scale = np.exp2(byte - 127.0)
    codes = (blocks / scale).astype(np.float32).astype(dtype).astype(np.float64)
    return np.moveaxis((codes * scale).reshape(v.shape), -1, axis)


WIDE = False


def mx_kscale(k):
    if not WIDE:
        return np.ones(k)
    levels = np.array([10, -10, 5, -5, 0])
    if k % 512:
        return np.exp2(np.random.permutation(np.resize(levels, k // 32))).repeat(32)
    a = np.empty((k // 512, 16))
    for p in range(k // 512):
        a[p, :8] = np.random.permutation(np.resize(levels, 8))
        for g in range(8):
            far = levels[np.abs(levels - a[p, g]) >= 10]
            a[p, g + 8] = far[np.random.randint(len(far))]
    return np.exp2(a.ravel()).repeat(32)


def f64(x):
    return np.asarray(x).astype(np.float64)


def striped(idx):
    return np.tile(idx.reshape(-1, 16).T, (8, 1)).astype(np.uint16)


def unstriped(offs):
    return offs[:16].T.reshape(-1).astype(np.int64)


def pack_weight(w):
    k, n = w.shape
    w = f64(np.asarray(w, np.float32).astype(ml_dtypes.bfloat16)).reshape(k // 32, 32, n)
    amax = np.abs(w).max(1)
    byte = np.clip(np.where(amax > 0, np.frexp(amax)[1] - 1 + 127 - 7, 1), 1, 254)
    scaled = (w * np.exp2(127.0 - byte)[:, None, :]).reshape(k, n).astype(np.float32)
    words = np.ascontiguousarray(scaled.reshape(k // 512, 128, 4, n).transpose(0, 1, 3, 2)).astype(ml_dtypes.float8_e4m3fn).view(np.uint8)
    return words, np.ascontiguousarray(byte.astype(np.uint8).reshape(k // 512, 16, n))


def unpack_weight(words, scales):
    g, p, n, _ = words.shape
    vals = np.ascontiguousarray(words).view(ml_dtypes.float8_e4m3fn).astype(np.float64) * np.repeat(np.exp2(scales.astype(np.float64) - 127.0), 8, axis=1)[..., None]
    return vals.transpose(0, 1, 3, 2).reshape(g * 512, n)


E2M1 = np.array([0.0, 0.5, 1.0, 1.5, 2.0, 3.0, 4.0, 6.0, -0.0, -0.5, -1.0, -1.5, -2.0, -3.0, -4.0, -6.0])


def pack_fp4(w):
    k, n = w.shape
    w = f64(np.asarray(w, np.float32).astype(ml_dtypes.bfloat16)).reshape(k // 32, 32, n)
    amax = np.abs(w).max(1)
    mant, ex = np.frexp(amax / 6.0)
    byte = np.clip(np.where(amax > 0, np.where(mant > 0.5, ex, ex - 1) + 127, 1), 1, 254)
    scaled = (w * np.exp2(127.0 - byte)[:, None, :]).reshape(k, n).astype(np.float32)
    c = np.ascontiguousarray(scaled.reshape(k // 512, 128, 4, n).transpose(0, 1, 3, 2)).astype(ml_dtypes.float4_e2m1fn).view(np.uint8) & 0xF
    words = (c[..., 0::2] | (c[..., 1::2] << 4)).reshape(k // 512, 128, 2 * n)
    return np.ascontiguousarray(words), np.ascontiguousarray(byte.astype(np.uint8).reshape(k // 512, 16, n))


def unpack_fp4(words, scales):
    g, _, n = scales.shape
    words = np.ascontiguousarray(words).reshape(g, 128, n, 2)
    nib = np.empty((g, 128, n, 4), np.uint8)
    nib[..., 0::2] = words & 0xF
    nib[..., 1::2] = words >> 4
    vals = E2M1[nib] * np.repeat(np.exp2(scales.astype(np.float64) - 127.0), 8, axis=1)[..., None]
    return vals.transpose(0, 1, 3, 2).reshape(g * 512, n)


K, T, S, D, V, H, N = 1024, 2048, 1024, 3, 512, 512, 128
P = 2 ** 7


def setup_inputs():
    n = np.random.standard_normal
    s = mx_kscale(K)[:, None]
    u = mx_kscale(H)
    packed_xT = pack_weight(n((K, T)) * s)
    packed_w2 = pack_fp4(n((H, N)) / np.sqrt(H) / u[:, None])
    return {
        "x_words": packed_xT[0],
        "x_scales": packed_xT[1],
        "w1": (n((K, H)) / np.sqrt(K) / s * u).astype(np.float32),
        "w2_words": packed_w2[0],
        "w2_scales": packed_w2[1],
        "gate": (np.tile(np.random.uniform(0.2, 1.0, (D, 1, V)) / np.sqrt(D), (1, P, 1))).astype(np.float32),
        "offs": striped(np.random.permutation(T)[:S]),
        "cen": striped(np.random.permutation(S)[:V]),
        "pos1": striped(np.random.permutation(S)[:V]),
        "pos2": striped(np.random.permutation(S)[:V]),
        "pos3": striped(np.random.permutation(S)[:V]),
    }


def reference(x_words, x_scales, w1, w2_words, w2_scales, gate, offs, cen, pos1, pos2, pos3):
    xq = unpack_weight(x_words, x_scales)[:, unstriped(offs)]
    h = mxq(f64(w1), 0, "e4m3").T @ xq
    z = h[:, unstriped(cen)] - (h[:, unstriped(pos1)] * f64(gate)[0, :1] + h[:, unstriped(pos2)] * f64(gate)[1, :1] + h[:, unstriped(pos3)] * f64(gate)[2, :1])
    return unpack_fp4(w2_words, w2_scales).T @ mxq(z, 0, "e4m3")

@@ -1,0 +1,230 @@
+from contextlib import ExitStack
+
+import concourse.mybir as mybir
+from concourse.masks import make_identity
+
+K, T, S, D, V, H, N = 1024, 2048, 1024, 3, 512, 512, 128
+FLOPS = 2 * K * H * S + 2 * H * N * V
+
+F32 = mybir.dt.float32
+BF16 = mybir.dt.bfloat16
+I32 = mybir.dt.int32
+U32 = mybir.dt.uint32
+U16 = mybir.dt.uint16
+U8 = mybir.dt.uint8
+FP8X4 = mybir.dt.float8_e4m3fn_x4
+FP4X4 = mybir.dt.float4_e2m1fn_x4
+MULT = mybir.AluOpType.mult
+SUBTRACT = mybir.AluOpType.subtract
+COPY = mybir.ActivationFunctionType.Copy
+
+P = 128
+PACK = 4
+K_PASS = P * PACK
+PASSES = K // K_PASS
+TILES = H // P
+BLOCKS = V // P
+PIECES = ((0, 512), (512, 768), (768, 1024))
+LAST_CHUNKS = ((0, 3), (3, 4))
+UNITS = ((0, 2), (2, 3), (3, 4))
+
+
+def tile_picked_lapl_none_p_kernel(tc, x_words, x_scales, w1, w2_words, w2_scales, gate, offs, cen, pos1, pos2, pos3, out):
+    nc = tc.nc
+    with ExitStack() as ctx:
+        keep = ctx.enter_context(tc.tile_pool(name="keep", bufs=1))
+        psum = ctx.enter_context(tc.psum_pool(name="psum", bufs=1))
+
+        def bank(tag, shape, name):
+            return psum.tile(shape, F32, name=name, tag=tag)
+
+        xs = keep.tile([P, T], U8, name="xs", align_bytes=64)
+        nc.vector.memset(xs[:].bitcast(I32), 0)
+        gate_rows = keep.tile([P, P], F32, name="gate_rows")
+        nc.vector.memset(gate_rows[:], 0.0)
+        w2s = keep.tile([P, N], U8, name="w2s", align_bytes=64)
+        nc.vector.memset(w2s[:].bitcast(I32), 0)
+        ident = keep.tile([P, P], F32, name="ident")
+        make_identity(nc, ident[:])
+
+        def load_list(src, name):
+            t = keep.tile(list(src.shape), U16, name=name)
+            nc.sync.dma_start(t[:], src)
+            return t
+
+        def load_words(z):
+            t = keep.tile([P, T], I32, name="xw%d" % z, align_bytes=64)
+            nc.sync.dma_start(t[:], x_words[z].rearrange("p n t -> p (n t)").bitcast(I32))
+            return t
+
+        def load_w1(z, c0, c1):
+            t = keep.tile([P, PACK, c1 - c0], F32, name="w1raw%d_%d" % (z, c0))
+            nc.sync.dma_start(t[:], w1[z * K_PASS:(z + 1) * K_PASS, c0:c1].rearrange("(p j) c -> p j c", j=PACK))
+            return t
+
+        offs_t = load_list(offs, "offs_t")
+        for q in range(4):
+            nc.sync.dma_start(xs[32 * q:32 * q + 4 * PASSES, :].bitcast(I32), x_scales[:, 4 * q:4 * q + 4, :].bitcast(I32))
+        nc.scalar.dma_start(gate_rows[0:D * BLOCKS, :], gate[:, 0, :].rearrange("d (b n) -> d b n", n=P))
+        xw = [load_words(0)]
+        raw = {(0, 0): load_w1(0, 0, P)[:]}
+        xw.append(load_words(1))
+        raw[0, 1] = load_w1(1, 0, P)[:]
+        pos1_t = load_list(pos1, "pos1_t")
+        pos2_t = load_list(pos2, "pos2_t")
+        cen_t = load_list(cen, "cen_t")
+        pos3_t = load_list(pos3, "pos3_t")
+        for z in range(PASSES):
+            raw[1, z] = load_w1(z, P, 2 * P)[:]
+        for z in range(PASSES):
+            rest = load_w1(z, 2 * P, H)
+            raw[2, z] = rest[:, :, 0:P]
+            raw[3, z] = rest[:, :, P:2 * P]
+        w2w = keep.tile([P, 2 * N], U8, name="w2w", align_bytes=64)
+        nc.sync.dma_start(w2w[:].bitcast(I32), w2_words[0].bitcast(I32))
+        for q in range(4):
+            nc.sync.dma_start(w2s[32 * q:32 * q + 4, :].bitcast(I32), w2_scales[0, 4 * q:4 * q + 4, :].bitcast(I32))
+
+        turned = bank("zt3", [P, P], "turned")
+        nc.tensor.transpose(turned[:], gate_rows[:], ident[:])
+        gate_cols = keep.tile([P, D * BLOCKS], F32, name="gate_cols")
+        nc.scalar.copy(gate_cols[:, 0:BLOCKS], turned[:, 0:BLOCKS])
+        nc.scalar.activation(gate_cols[:, BLOCKS:D * BLOCKS], turned[:, BLOCKS:D * BLOCKS], COPY, scale=-1.0)
+        gates = []
+        for d in range(D):
+            spread = bank("zt%d" % d, [P, V], "spread%d" % d)
+            for b in range(BLOCKS):
+                col = d * BLOCKS + b
+                nc.tensor.transpose(spread[:, b * P:(b + 1) * P], gate_cols[:, col:col + 1].to_broadcast([P, P]), ident[:])
+            g = keep.tile([P, V], F32, name="gate%d" % d)
+            nc.scalar.copy(g[:], spread[:])
+            gates.append(g)
+
+        def cast_w1(dst, src):
+            nc.scalar.copy(dst.rearrange("p (c i j) -> p c j i", i=4, j=PACK), src.rearrange("p j (c i) -> p c j i", i=4))
+
+        gs = keep.tile([P, S], U8, name="gs", align_bytes=64)
+        nc.vector.tensor_copy(gs[:], xs[:].indirect(offs_t[:]))
+        gw0 = keep.tile([P, S], U32, name="gw0", align_bytes=64)
+        nc.vector.tensor_copy(gw0[:], xw[0][:].bitcast(U32).indirect(offs_t[:]))
+        picked = {(0, a): gw0[:, a:b] for a, b in PIECES}
+
+        codes = keep.tile([P, PASSES * P], U32, name="codes0", tag="chain0", align_bytes=64)
+        plane = keep.tile([P, PASSES * P], U8, name="plane0", align_bytes=64)
+        for z in range(PASSES):
+            staged = keep.tile([P, K_PASS], BF16, name="staged0_%d" % z, tag="first%d" % z, align_bytes=64)
+            cast_w1(staged[:], raw[0, z])
+            if z == 1:
+                for a, b in PIECES[:-1]:
+                    t = keep.tile([P, b - a], U32, name="gw1_%d" % a, align_bytes=64)
+                    nc.vector.tensor_copy(t[:], xw[1][:].bitcast(U32).indirect(offs_t[:, a // 16:b // 16]))
+                    picked[1, a] = t[:]
+            nc.vector.quantize_mx(out=codes[:, z * P:(z + 1) * P].bitcast(FP8X4), scales=plane[:, z * P:(z + 1) * P], in_=staged[:])
+        a, b = PIECES[-1]
+        t = keep.tile([P, b - a], U32, name="gw1_%d" % a, tag="first1", align_bytes=64)
+        nc.vector.tensor_copy(t[:], xw[1][:].bitcast(U32).indirect(offs_t[:, a // 16:b // 16]))
+        picked[1, a] = t[:]
+
+        def mx_pass(acc, codes, plane, z, a, b):
+            nc.tensor.matmul_mx(
+                out=acc,
+                lhsT=codes[:, z * P:(z + 1) * P].bitcast(FP8X4),
+                lhsT_scale=plane[:, z * P:(z + 1) * P],
+                rhs=picked[z, a].bitcast(FP8X4),
+                rhs_scale=gs[4 * z:P, a:b],
+                start=(z == 0),
+                stop=(z == PASSES - 1),
+            )
+
+        h = keep.tile([P, S], F32, name="h0")
+        accs = [bank(tag, [P, b - a], "acc0_%d" % a) for tag, (a, b) in zip(("h0", "h1", "h2"), PIECES)]
+        for z in range(PASSES):
+            for acc, (a, b) in zip(accs, PIECES):
+                mx_pass(acc[:], codes, plane, z, a, b)
+        for n, (acc, (a, b)) in enumerate(zip(accs, PIECES)):
+            if n == 0:
+                nc.scalar.copy(h[:, a:b], acc[:])
+            else:
+                nc.vector.tensor_copy(h[:, a:b], acc[:])
+
+        def stage(tile_no):
+            staged = keep.tile([P, PASSES * K_PASS], BF16, name="staged%d" % tile_no, tag="chain%d" % (tile_no - 1), align_bytes=64)
+            for z in range(PASSES):
+                cast_w1(staged[:, z * K_PASS:(z + 1) * K_PASS], raw[tile_no, z])
+            return staged
+
+        def project(tile_no, staged):
+            codes = keep.tile([P, PASSES * P], U32, name="codes%d" % tile_no, tag="chain%d" % tile_no, align_bytes=64)
+            plane = keep.tile([P, PASSES * P], U8, name="plane%d" % tile_no, align_bytes=64)
+            nc.vector.quantize_mx(out=codes[:].bitcast(FP8X4), scales=plane[:], in_=staged[:])
+            h_next = keep.tile([P, S], F32, name="h%d" % tile_no)
+            tags = ("h3", "h0") if tile_no % 2 else ("h1", "h2")
+            for half in range(2):
+                acc = bank(tags[half], [P, 512], "acc%d_%d" % (tile_no, half))
+                for a, b in PIECES:
+                    if a // 512 == half:
+                        for z in range(PASSES):
+                            mx_pass(acc[:, a - 512 * half:b - 512 * half], codes, plane, z, a, b)
+                nc.scalar.copy(h_next[:, 512 * half:512 * (half + 1)], acc[:])
+            return h_next
+
+        zb = [keep.tile([P, 2, P, 2], BF16, name="zb%d" % b, align_bytes=64) for b in range(BLOCKS)]
+        staged = stage(1)
+        for tile_no in range(TILES):
+            last = tile_no == TILES - 1
+            first_term = keep.tile([P, V], F32, name="first_term%d" % tile_no)
+            chunks = LAST_CHUNKS if last else ((0, BLOCKS),)
+            c0, c1 = chunks[0][0] * P, chunks[0][1] * P
+            nc.vector.tensor_tensor(first_term[:, c0:c1], h[:].indirect(pos1_t[:, c0 // 16:c1 // 16]), gates[0][:, c0:c1], MULT)
+            if not last:
+                h_next = project(tile_no + 1, staged)
+                if tile_no + 2 < TILES:
+                    staged = stage(tile_no + 2)
+            terms = keep.tile([P, 3, V], F32, name="terms%d" % tile_no, tag="chain%d" % tile_no, align_bytes=64)
+            for n, (b0, b1) in enumerate(chunks):
+                c0, c1 = b0 * P, b1 * P
+                cols = slice(c0 // 16, c1 // 16)
+                if n > 0:
+                    nc.vector.tensor_tensor(first_term[:, c0:c1], h[:].indirect(pos1_t[:, cols]), gates[0][:, c0:c1], MULT)
+                sums = [bank("zt%d" % b, [P, P], "sum%d_%d" % (tile_no, b)) for b in range(b0, b1)]
+                steps = (
+                    (pos2_t, gates[1], MULT),
+                    (cen_t, first_term, SUBTRACT),
+                    (pos3_t, gates[2], MULT),
+                )
+                for s, (lst, other, op) in enumerate(steps):
+                    nc.vector.tensor_tensor(terms[:, s, c0:c1], h[:].indirect(lst[:, cols]), other[:, c0:c1], op)
+                    for b in range(b0, b1):
+                        nc.tensor.matmul(sums[b - b0][:], terms[:, s, b * P:(b + 1) * P], ident[:], start=(s == 0), stop=(s == 2), is_transpose=True)
+                for b in range(b0, b1):
+                    nc.scalar.copy(zb[b][:, :, 32 * tile_no:32 * (tile_no + 1), :], sums[b - b0][:].rearrange("v (q u e) -> v u q e", u=2, e=2))
+            if not last:
+                h = h_next
+
+        result = keep.tile([P, V], F32, name="result")
+        out_a = bank("h0", [P, 3 * P], "out_a")
+        out_c = bank("zt0", [P, P], "out_c")
+        for n, (b0, b1) in enumerate(UNITS):
+            nb = b1 - b0
+            back = bank("h%d" % (n + 1), [P, nb, 2, P], "back%d" % n)
+            for b in range(b0, b1):
+                words = zb[b][:].rearrange("v u p e -> v (u p e)").bitcast(F32)
+                for u in range(2):
+                    nc.tensor.transpose(back[:, b - b0, u, :], words[:, u * P:(u + 1) * P], ident[:])
+            zq = keep.tile([P, nb * K_PASS], BF16, name="zq%d" % n, align_bytes=64)
+            dst = zq[:].bitcast(F32).rearrange("p (b v u) -> p b v u", b=nb, u=2)
+            src = back[:].rearrange("p b u v -> p b v u")
+            if n < len(UNITS) - 1:
+                nc.vector.tensor_copy(dst, src)
+            else:
+                nc.scalar.copy(dst, src)
+            zc = keep.tile([P, nb * P], U32, name="zc%d" % n, align_bytes=64)
+            zs = keep.tile([P, nb * P], U8, name="zs%d" % n, align_bytes=64)
+            nc.vector.quantize_mx(out=zc[:].bitcast(FP8X4), scales=zs[:], in_=zq[:])
+            acc = out_a[:, b0 * P:b1 * P] if n < len(UNITS) - 1 else out_c[:]
+            nc.tensor.matmul_mx(out=acc, lhsT=w2w[:].bitcast(FP4X4), lhsT_scale=w2s[:], rhs=zc[:].bitcast(FP8X4), rhs_scale=zs[:], start=True, stop=True)
+            if n == 1:
+                nc.scalar.copy(result[:, 0:3 * P], out_a[:])
+                nc.sync.dma_start(out[:, 0:3 * P], result[:, 0:3 * P])
+        nc.vector.tensor_copy(result[:, 3 * P:V], out_c[:])
+        nc.scalar.dma_start(out[:, 3 * P:V], result[:, 3 * P:V])

@@ -15,7 +15,6 @@ U8 = mybir.dt.uint8
 FP8X4 = mybir.dt.float8_e4m3fn_x4
 FP4X4 = mybir.dt.float4_e2m1fn_x4
 MULT = mybir.AluOpType.mult
-SUBTRACT = mybir.AluOpType.subtract
 COPY = mybir.ActivationFunctionType.Copy
 
 P = 128
@@ -24,9 +23,14 @@ K_PASS = P * PACK
 PASSES = K // K_PASS
 TILES = H // P
 BLOCKS = V // P
+QUADRANT = 32
+QUADRANTS = P // QUADRANT
+ROWS = 4
+PER_COLUMN = 16
+BANK = 512
+ALIGN = 64
 PIECES = ((0, 512), (512, 768), (768, 1024))
-LAST_CHUNKS = ((0, 3), (3, 4))
-UNITS = ((0, 2), (2, 3), (3, 4))
+RUNS = ((0, 2), (2, 3), (3, 4))
 
 
 def tile_picked_lapl_none_p_kernel(tc, x_words, x_scales, w1, w2_words, w2_scales, gate, offs, cen, pos1, pos2, pos3, out):
@@ -38,193 +42,220 @@ def tile_picked_lapl_none_p_kernel(tc, x_words, x_scales, w1, w2_words, w2_scale
         def bank(tag, shape, name):
             return psum.tile(shape, F32, name=name, tag=tag)
 
-        xs = keep.tile([P, T], U8, name="xs", align_bytes=64)
-        nc.vector.memset(xs[:].bitcast(I32), 0)
+        def entries(list_tile, a, b):
+            return list_tile[:, a // PER_COLUMN:b // PER_COLUMN]
+
+        xs = keep.tile([P, T], U8, name="xs", align_bytes=ALIGN)
+        nc.vector.memset(xs[:, 0:T // 2].bitcast(I32), 0)
+        nc.gpsimd.memset(xs[:, T // 2:T].bitcast(I32), 0)
         gate_rows = keep.tile([P, P], F32, name="gate_rows")
-        nc.vector.memset(gate_rows[:], 0.0)
-        w2s = keep.tile([P, N], U8, name="w2s", align_bytes=64)
+        nc.gpsimd.memset(gate_rows[:], 0.0)
+        w2s = keep.tile([P, N], U8, name="w2s", align_bytes=ALIGN)
         nc.vector.memset(w2s[:].bitcast(I32), 0)
         ident = keep.tile([P, P], F32, name="ident")
         make_identity(nc, ident[:])
 
         def load_list(src, name):
-            t = keep.tile(list(src.shape), U16, name=name)
-            nc.sync.dma_start(t[:], src)
-            return t
+            list_tile = keep.tile(list(src.shape), U16, name=name)
+            nc.sync.dma_start(list_tile[:], src)
+            return list_tile
 
-        def load_words(z):
-            t = keep.tile([P, T], I32, name="xw%d" % z, align_bytes=64)
-            nc.sync.dma_start(t[:], x_words[z].rearrange("p n t -> p (n t)").bitcast(I32))
-            return t
+        def load_words(g):
+            table = keep.tile([P, T], I32, name="xw%d" % g, align_bytes=ALIGN)
+            nc.sync.dma_start(table[:], x_words[g].rearrange("p n t -> p (n t)").bitcast(I32))
+            return table
 
-        def load_w1(z, c0, c1):
-            t = keep.tile([P, PACK, c1 - c0], F32, name="w1raw%d_%d" % (z, c0))
-            nc.sync.dma_start(t[:], w1[z * K_PASS:(z + 1) * K_PASS, c0:c1].rearrange("(p j) c -> p j c", j=PACK))
-            return t
+        def load_w1(tile_no, g):
+            rows = keep.tile([P, PACK, P], F32, name="w1raw%d_%d" % (tile_no, g), tag="raw%d_%d" % (tile_no, g))
+            src = w1[g * K_PASS:(g + 1) * K_PASS, tile_no * P:(tile_no + 1) * P]
+            nc.sync.dma_start(rows[:], src.rearrange("(p t) c -> p t c", t=PACK))
+            return rows[:]
 
         offs_t = load_list(offs, "offs_t")
-        for q in range(4):
-            nc.sync.dma_start(xs[32 * q:32 * q + 4 * PASSES, :].bitcast(I32), x_scales[:, 4 * q:4 * q + 4, :].bitcast(I32))
-        nc.scalar.dma_start(gate_rows[0:D * BLOCKS, :], gate[:, 0, :].rearrange("d (b n) -> d b n", n=P))
-        xw = [load_words(0)]
-        raw = {(0, 0): load_w1(0, 0, P)[:]}
-        xw.append(load_words(1))
-        raw[0, 1] = load_w1(1, 0, P)[:]
-        pos1_t = load_list(pos1, "pos1_t")
-        pos2_t = load_list(pos2, "pos2_t")
         cen_t = load_list(cen, "cen_t")
-        pos3_t = load_list(pos3, "pos3_t")
-        for z in range(PASSES):
-            raw[1, z] = load_w1(z, P, 2 * P)[:]
-        for z in range(PASSES):
-            rest = load_w1(z, 2 * P, H)
-            raw[2, z] = rest[:, :, 0:P]
-            raw[3, z] = rest[:, :, P:2 * P]
-        w2w = keep.tile([P, 2 * N], U8, name="w2w", align_bytes=64)
+        for q in range(QUADRANTS):
+            rows_q = xs[QUADRANT * q:QUADRANT * q + ROWS * PASSES, :]
+            nc.sync.dma_start(rows_q.bitcast(I32), x_scales[:, ROWS * q:ROWS * (q + 1), :].bitcast(I32))
+        xw = [load_words(0)]
+        nc.sync.dma_start(gate_rows[0:D * BLOCKS, :], gate[:, 0, :].rearrange("d (b n) -> d b n", n=P))
+        raw = {(0, 0): load_w1(0, 0)}
+        xw.append(load_words(1))
+        raw[0, 1] = load_w1(0, 1)
+        neighbours = [load_list(src, name) for src, name in ((pos1, "pos1_t"), (pos2, "pos2_t"), (pos3, "pos3_t"))]
+        for tile_no in range(1, TILES):
+            for g in range(PASSES):
+                raw[tile_no, g] = load_w1(tile_no, g)
+        w2w = keep.tile([P, 2 * N], U8, name="w2w", align_bytes=ALIGN)
         nc.sync.dma_start(w2w[:].bitcast(I32), w2_words[0].bitcast(I32))
-        for q in range(4):
-            nc.sync.dma_start(w2s[32 * q:32 * q + 4, :].bitcast(I32), w2_scales[0, 4 * q:4 * q + 4, :].bitcast(I32))
+        for q in range(QUADRANTS):
+            rows_q = w2s[QUADRANT * q:QUADRANT * q + ROWS, :]
+            nc.sync.dma_start(rows_q.bitcast(I32), w2_scales[0, ROWS * q:ROWS * (q + 1), :].bitcast(I32))
+
+        def round_w1(dst, src):
+            nc.scalar.copy(dst.rearrange("p (c t) -> p c t", t=PACK), src.rearrange("p t c -> p c t"))
+
+        gs = keep.tile([P, S], U8, name="gs", align_bytes=ALIGN)
+        nc.vector.tensor_copy(gs[:], xs[:].indirect(offs_t[:]))
+        gw0 = keep.tile([P, S], U32, name="gw0", align_bytes=ALIGN)
+        nc.vector.tensor_copy(gw0[:], xw[0][:].bitcast(U32).indirect(offs_t[:]))
+        picked = {(0, a): gw0[:, a:b] for a, b in PIECES}
+
+        def pick_second_pass(a, b, tag):
+            words = keep.tile([P, b - a], U32, name="gw1_%d" % a, tag=tag, align_bytes=ALIGN)
+            nc.vector.tensor_copy(words[:], xw[1][:].bitcast(U32).indirect(entries(offs_t, a, b)))
+            picked[1, a] = words[:]
+
+        codes0 = keep.tile([P, PASSES * P], U32, name="codes0", align_bytes=ALIGN)
+        scales0 = keep.tile([P, PASSES * P], U8, name="scales0", align_bytes=ALIGN)
+
+        def quantise_first_tile(g):
+            rounded = keep.tile([P, K_PASS], BF16, name="rounded0_%d" % g, tag="first%d" % g, align_bytes=ALIGN)
+            round_w1(rounded[:], raw[0, g])
+            cols = slice(g * P, (g + 1) * P)
+            nc.vector.quantize_mx(out=codes0[:, cols].bitcast(FP8X4), scales=scales0[:, cols], in_=rounded[:])
+
+        quantise_first_tile(0)
 
         turned = bank("zt3", [P, P], "turned")
         nc.tensor.transpose(turned[:], gate_rows[:], ident[:])
         gate_cols = keep.tile([P, D * BLOCKS], F32, name="gate_cols")
-        nc.scalar.copy(gate_cols[:, 0:BLOCKS], turned[:, 0:BLOCKS])
-        nc.scalar.activation(gate_cols[:, BLOCKS:D * BLOCKS], turned[:, BLOCKS:D * BLOCKS], COPY, scale=-1.0)
-        gates = []
+        nc.scalar.activation(gate_cols[:], turned[:, 0:D * BLOCKS], COPY, scale=-1.0)
+        minus_gates = []
         for d in range(D):
             spread = bank("zt%d" % d, [P, V], "spread%d" % d)
-            for b in range(BLOCKS):
-                col = d * BLOCKS + b
-                nc.tensor.transpose(spread[:, b * P:(b + 1) * P], gate_cols[:, col:col + 1].to_broadcast([P, P]), ident[:])
-            g = keep.tile([P, V], F32, name="gate%d" % d)
-            nc.scalar.copy(g[:], spread[:])
-            gates.append(g)
+            for blk in range(BLOCKS):
+                col = d * BLOCKS + blk
+                nc.tensor.transpose(spread[:, blk * P:(blk + 1) * P], gate_cols[:, col:col + 1].to_broadcast([P, P]), ident[:])
+            minus_gate = keep.tile([P, V], F32, name="minus_gate%d" % d)
+            nc.scalar.copy(minus_gate[:], spread[:])
+            minus_gates.append(minus_gate)
 
-        def cast_w1(dst, src):
-            nc.scalar.copy(dst.rearrange("p (c i j) -> p c j i", i=4, j=PACK), src.rearrange("p j (c i) -> p c j i", i=4))
+        for a, b in PIECES[:-1]:
+            pick_second_pass(a, b, "gw1_%d" % a)
+        quantise_first_tile(1)
+        pick_second_pass(PIECES[-1][0], PIECES[-1][1], "first1")
 
-        gs = keep.tile([P, S], U8, name="gs", align_bytes=64)
-        nc.vector.tensor_copy(gs[:], xs[:].indirect(offs_t[:]))
-        gw0 = keep.tile([P, S], U32, name="gw0", align_bytes=64)
-        nc.vector.tensor_copy(gw0[:], xw[0][:].bitcast(U32).indirect(offs_t[:]))
-        picked = {(0, a): gw0[:, a:b] for a, b in PIECES}
-
-        codes = keep.tile([P, PASSES * P], U32, name="codes0", tag="chain0", align_bytes=64)
-        plane = keep.tile([P, PASSES * P], U8, name="plane0", align_bytes=64)
-        for z in range(PASSES):
-            staged = keep.tile([P, K_PASS], BF16, name="staged0_%d" % z, tag="first%d" % z, align_bytes=64)
-            cast_w1(staged[:], raw[0, z])
-            if z == 1:
-                for a, b in PIECES[:-1]:
-                    t = keep.tile([P, b - a], U32, name="gw1_%d" % a, align_bytes=64)
-                    nc.vector.tensor_copy(t[:], xw[1][:].bitcast(U32).indirect(offs_t[:, a // 16:b // 16]))
-                    picked[1, a] = t[:]
-            nc.vector.quantize_mx(out=codes[:, z * P:(z + 1) * P].bitcast(FP8X4), scales=plane[:, z * P:(z + 1) * P], in_=staged[:])
-        a, b = PIECES[-1]
-        t = keep.tile([P, b - a], U32, name="gw1_%d" % a, tag="first1", align_bytes=64)
-        nc.vector.tensor_copy(t[:], xw[1][:].bitcast(U32).indirect(offs_t[:, a // 16:b // 16]))
-        picked[1, a] = t[:]
-
-        def mx_pass(acc, codes, plane, z, a, b):
+        def mx_pass(acc, codes, scales, g, a, b):
             nc.tensor.matmul_mx(
                 out=acc,
-                lhsT=codes[:, z * P:(z + 1) * P].bitcast(FP8X4),
-                lhsT_scale=plane[:, z * P:(z + 1) * P],
-                rhs=picked[z, a].bitcast(FP8X4),
-                rhs_scale=gs[4 * z:P, a:b],
-                start=(z == 0),
-                stop=(z == PASSES - 1),
+                lhsT=codes[:, g * P:(g + 1) * P].bitcast(FP8X4),
+                lhsT_scale=scales[:, g * P:(g + 1) * P],
+                rhs=picked[g, a].bitcast(FP8X4),
+                rhs_scale=gs[ROWS * g:P, a:b],
+                start=(g == 0),
+                stop=(g == PASSES - 1),
             )
 
         h = keep.tile([P, S], F32, name="h0")
-        accs = [bank(tag, [P, b - a], "acc0_%d" % a) for tag, (a, b) in zip(("h0", "h1", "h2"), PIECES)]
-        for z in range(PASSES):
+        accs = [bank("h%d" % n, [P, b - a], "acc0_%d" % a) for n, (a, b) in enumerate(PIECES)]
+        for g in range(PASSES):
             for acc, (a, b) in zip(accs, PIECES):
-                mx_pass(acc[:], codes, plane, z, a, b)
-        for n, (acc, (a, b)) in enumerate(zip(accs, PIECES)):
-            if n == 0:
+                mx_pass(acc[:], codes0, scales0, g, a, b)
+        for acc, (a, b) in zip(accs, PIECES):
+            if a == 0:
                 nc.scalar.copy(h[:, a:b], acc[:])
             else:
                 nc.vector.tensor_copy(h[:, a:b], acc[:])
 
-        def stage(tile_no):
-            staged = keep.tile([P, PASSES * K_PASS], BF16, name="staged%d" % tile_no, tag="chain%d" % (tile_no - 1), align_bytes=64)
-            for z in range(PASSES):
-                cast_w1(staged[:, z * K_PASS:(z + 1) * K_PASS], raw[tile_no, z])
-            return staged
+        def round_tile(tile_no):
+            rounded = keep.tile([P, PASSES * K_PASS], BF16, name="rounded%d" % tile_no, tag="rounded%d" % tile_no, align_bytes=ALIGN)
+            for g in range(PASSES):
+                round_w1(rounded[:, g * K_PASS:(g + 1) * K_PASS], raw[tile_no, g])
+            return rounded
 
-        def project(tile_no, staged):
-            codes = keep.tile([P, PASSES * P], U32, name="codes%d" % tile_no, tag="chain%d" % tile_no, align_bytes=64)
-            plane = keep.tile([P, PASSES * P], U8, name="plane%d" % tile_no, align_bytes=64)
-            nc.vector.quantize_mx(out=codes[:].bitcast(FP8X4), scales=plane[:], in_=staged[:])
-            h_next = keep.tile([P, S], F32, name="h%d" % tile_no)
+        def project(tile_no, rounded):
+            codes = keep.tile([P, PASSES * P], U32, name="codes%d" % tile_no, align_bytes=ALIGN)
+            scales = keep.tile([P, PASSES * P], U8, name="scales%d" % tile_no, align_bytes=ALIGN)
+            nc.vector.quantize_mx(out=codes[:].bitcast(FP8X4), scales=scales[:], in_=rounded[:])
+            h_tile = keep.tile([P, S], F32, name="h%d" % tile_no, tag="raw%d_1" % (tile_no + 1))
             tags = ("h3", "h0") if tile_no % 2 else ("h1", "h2")
-            for half in range(2):
-                acc = bank(tags[half], [P, 512], "acc%d_%d" % (tile_no, half))
+            for half in range(S // BANK):
+                acc = bank(tags[half], [P, BANK], "acc%d_%d" % (tile_no, half))
                 for a, b in PIECES:
-                    if a // 512 == half:
-                        for z in range(PASSES):
-                            mx_pass(acc[:, a - 512 * half:b - 512 * half], codes, plane, z, a, b)
-                nc.scalar.copy(h_next[:, 512 * half:512 * (half + 1)], acc[:])
-            return h_next
+                    if a // BANK == half:
+                        for g in range(PASSES):
+                            mx_pass(acc[:, a - BANK * half:b - BANK * half], codes, scales, g, a, b)
+                nc.scalar.copy(h_tile[:, BANK * half:BANK * (half + 1)], acc[:])
+            return h_tile
 
-        zb = [keep.tile([P, 2, P, 2], BF16, name="zb%d" % b, align_bytes=64) for b in range(BLOCKS)]
-        staged = stage(1)
+        zb = [keep.tile([P, 2, P, 2], BF16, name="zb%d" % blk, tag="zb%d" % blk, align_bytes=ALIGN) for blk in range(BLOCKS)]
+        result = keep.tile([P, V], F32, name="result")
+
+        def turn_back(run, b0, b1):
+            back = bank("h%d" % (run + 1), [P, b1 - b0, 2, P], "back%d" % run)
+            for blk in range(b0, b1):
+                pairs = zb[blk][:].rearrange("v u p e -> v (u p e)").bitcast(F32)
+                for u in range(2):
+                    nc.tensor.transpose(back[:, blk - b0, u, :], pairs[:, u * P:(u + 1) * P], ident[:])
+            return back
+
+        def add_turned(total, term, start, stop):
+            nc.tensor.matmul(total, term, ident[:], start=start, stop=stop, is_transpose=True)
+
+        backs = []
+        rounded_tiles = {tile_no: round_tile(tile_no) for tile_no in range(1, TILES)}
         for tile_no in range(TILES):
             last = tile_no == TILES - 1
-            first_term = keep.tile([P, V], F32, name="first_term%d" % tile_no)
-            chunks = LAST_CHUNKS if last else ((0, BLOCKS),)
-            c0, c1 = chunks[0][0] * P, chunks[0][1] * P
-            nc.vector.tensor_tensor(first_term[:, c0:c1], h[:].indirect(pos1_t[:, c0 // 16:c1 // 16]), gates[0][:, c0:c1], MULT)
-            if not last:
-                h_next = project(tile_no + 1, staged)
-                if tile_no + 2 < TILES:
-                    staged = stage(tile_no + 2)
-            terms = keep.tile([P, 3, V], F32, name="terms%d" % tile_no, tag="chain%d" % tile_no, align_bytes=64)
-            for n, (b0, b1) in enumerate(chunks):
+            if 0 < tile_no < TILES - 1:
+                h_next = project(tile_no + 1, rounded_tiles[tile_no + 1])
+            centre = keep.tile([P, V], F32, name="centre%d" % tile_no)
+            runs = RUNS if last else ((0, BLOCKS),)
+            c0, c1 = runs[0][0] * P, runs[0][1] * P
+            nc.vector.tensor_copy(centre[:, c0:c1], h[:].indirect(entries(cen_t, c0, c1)))
+            if tile_no == 0:
+                h_next = project(1, rounded_tiles[1])
+            terms_tag = "rounded1" if tile_no == 0 else "terms%d" % tile_no
+            terms = keep.tile([P, D, V], F32, name="terms%d" % tile_no, tag=terms_tag, align_bytes=ALIGN)
+            for run, (b0, b1) in enumerate(runs):
                 c0, c1 = b0 * P, b1 * P
-                cols = slice(c0 // 16, c1 // 16)
-                if n > 0:
-                    nc.vector.tensor_tensor(first_term[:, c0:c1], h[:].indirect(pos1_t[:, cols]), gates[0][:, c0:c1], MULT)
-                sums = [bank("zt%d" % b, [P, P], "sum%d_%d" % (tile_no, b)) for b in range(b0, b1)]
-                steps = (
-                    (pos2_t, gates[1], MULT),
-                    (cen_t, first_term, SUBTRACT),
-                    (pos3_t, gates[2], MULT),
-                )
-                for s, (lst, other, op) in enumerate(steps):
-                    nc.vector.tensor_tensor(terms[:, s, c0:c1], h[:].indirect(lst[:, cols]), other[:, c0:c1], op)
-                    for b in range(b0, b1):
-                        nc.tensor.matmul(sums[b - b0][:], terms[:, s, b * P:(b + 1) * P], ident[:], start=(s == 0), stop=(s == 2), is_transpose=True)
-                for b in range(b0, b1):
-                    nc.scalar.copy(zb[b][:, :, 32 * tile_no:32 * (tile_no + 1), :], sums[b - b0][:].rearrange("v (q u e) -> v u q e", u=2, e=2))
+                if run > 0:
+                    nc.vector.tensor_copy(centre[:, c0:c1], h[:].indirect(entries(cen_t, c0, c1)))
+                sums = [bank("zt%d" % blk, [P, P], "sum%d_%d" % (tile_no, blk)) for blk in range(b0, b1)]
+                for blk in range(b0, b1):
+                    add_turned(sums[blk - b0][:], centre[:, blk * P:(blk + 1) * P], True, False)
+                for d in range(D):
+                    term = terms[:, d, c0:c1]
+                    if last and b1 == BLOCKS and d == D - 1:
+                        closing = keep.tile([P, c1 - c0], F32, name="closing", tag="zb0", align_bytes=ALIGN)
+                        term = closing[:]
+                    nc.vector.tensor_tensor(term, h[:].indirect(entries(neighbours[d], c0, c1)), minus_gates[d][:, c0:c1], MULT)
+                    for n in range(b1 - b0):
+                        add_turned(sums[n][:], term[:, n * P:(n + 1) * P], False, d == D - 1)
+                span = slice(P // PACK * tile_no, P // PACK * (tile_no + 1))
+                for blk in range(b0, b1):
+                    nc.scalar.copy(zb[blk][:, :, span, :], sums[blk - b0][:].rearrange("v (r u e) -> v u r e", u=2, e=2))
+                if last:
+                    backs.append(turn_back(run, b0, b1))
             if not last:
                 h = h_next
 
-        result = keep.tile([P, V], F32, name="result")
-        out_a = bank("h0", [P, 3 * P], "out_a")
-        out_c = bank("zt0", [P, P], "out_c")
-        for n, (b0, b1) in enumerate(UNITS):
-            nb = b1 - b0
-            back = bank("h%d" % (n + 1), [P, nb, 2, P], "back%d" % n)
-            for b in range(b0, b1):
-                words = zb[b][:].rearrange("v u p e -> v (u p e)").bitcast(F32)
-                for u in range(2):
-                    nc.tensor.transpose(back[:, b - b0, u, :], words[:, u * P:(u + 1) * P], ident[:])
-            zq = keep.tile([P, nb * K_PASS], BF16, name="zq%d" % n, align_bytes=64)
-            dst = zq[:].bitcast(F32).rearrange("p (b v u) -> p b v u", b=nb, u=2)
-            src = back[:].rearrange("p b u v -> p b v u")
-            if n < len(UNITS) - 1:
-                nc.vector.tensor_copy(dst, src)
-            else:
+        early = RUNS[-1][0] * P
+        out_early = bank("h0", [P, early], "out_early")
+        out_last = bank("zt0", [P, V - early], "out_last")
+        for run, (b0, b1) in enumerate(RUNS):
+            closing_run = run == len(RUNS) - 1
+            width = (b1 - b0) * P
+            zq = keep.tile([P, width * PACK], BF16, name="zq%d" % run, align_bytes=ALIGN)
+            dst = zq[:].bitcast(F32).rearrange("p (b v u) -> p b v u", b=b1 - b0, u=2)
+            src = backs[run][:].rearrange("p b u v -> p b v u")
+            if closing_run:
                 nc.scalar.copy(dst, src)
-            zc = keep.tile([P, nb * P], U32, name="zc%d" % n, align_bytes=64)
-            zs = keep.tile([P, nb * P], U8, name="zs%d" % n, align_bytes=64)
-            nc.vector.quantize_mx(out=zc[:].bitcast(FP8X4), scales=zs[:], in_=zq[:])
-            acc = out_a[:, b0 * P:b1 * P] if n < len(UNITS) - 1 else out_c[:]
-            nc.tensor.matmul_mx(out=acc, lhsT=w2w[:].bitcast(FP4X4), lhsT_scale=w2s[:], rhs=zc[:].bitcast(FP8X4), rhs_scale=zs[:], start=True, stop=True)
-            if n == 1:
-                nc.scalar.copy(result[:, 0:3 * P], out_a[:])
-                nc.sync.dma_start(out[:, 0:3 * P], result[:, 0:3 * P])
-        nc.vector.tensor_copy(result[:, 3 * P:V], out_c[:])
-        nc.scalar.dma_start(out[:, 3 * P:V], result[:, 3 * P:V])
+            else:
+                nc.vector.tensor_copy(dst, src)
+            z_codes = keep.tile([P, width], U32, name="z_codes%d" % run, align_bytes=ALIGN)
+            z_scales = keep.tile([P, width], U8, name="z_scales%d" % run, align_bytes=ALIGN)
+            nc.vector.quantize_mx(out=z_codes[:].bitcast(FP8X4), scales=z_scales[:], in_=zq[:])
+            nc.tensor.matmul_mx(
+                out=out_last[:] if closing_run else out_early[:, b0 * P:b1 * P],
+                lhsT=w2w[:].bitcast(FP4X4),
+                lhsT_scale=w2s[:],
+                rhs=z_codes[:].bitcast(FP8X4),
+                rhs_scale=z_scales[:],
+                start=True,
+                stop=True,
+            )
+            if b1 * P == early:
+                nc.scalar.copy(result[:, 0:early], out_early[:])
+                nc.sync.dma_start(out[:, 0:early], result[:, 0:early])
+        nc.vector.tensor_copy(result[:, early:V], out_last[:])
+        nc.scalar.dma_start(out[:, early:V], result[:, early:V])

@@ -31,6 +31,14 @@ BANK = 512
 ALIGN = 64
 PIECES = ((0, 512), (512, 768), (768, 1024))
 RUNS = ((0, 2), (2, 3), (3, 4))
+KIB = 1024
+WORDS_AT = (0, 8 * KIB)
+XS_AT = 35 * KIB
+FIRST_AT = (16 * KIB, 34 * KIB)
+GATES_AT = 18 * KIB
+RAW_AT = (None, 36 * KIB, 24 * KIB, 8 * KIB, 28 * KIB)
+PICKED_AT = 24 * KIB - S // 2
+W2_AT = 14 * KIB
 
 
 def tile_picked_lapl_none_p_kernel(tc, x_words, x_scales, w1, w2_words, w2_scales, gate, offs, cen, pos1, pos2, pos3, out):
@@ -38,6 +46,7 @@ def tile_picked_lapl_none_p_kernel(tc, x_words, x_scales, w1, w2_words, w2_scale
     with ExitStack() as ctx:
         keep = ctx.enter_context(tc.tile_pool(name="keep", bufs=1))
         psum = ctx.enter_context(tc.psum_pool(name="psum", bufs=1))
+        placed = ctx.enter_context(tc.tile_pool(name="placed", bufs=1))
 
         def bank(tag, shape, name):
             return psum.tile(shape, F32, name=name, tag=tag)
@@ -45,15 +54,15 @@ def tile_picked_lapl_none_p_kernel(tc, x_words, x_scales, w1, w2_words, w2_scale
         def entries(list_tile, a, b):
             return list_tile[:, a // PER_COLUMN:b // PER_COLUMN]
 
-        xs = keep.tile([P, T], U8, name="xs", align_bytes=ALIGN)
-        nc.vector.memset(xs[:, 0:T // 2].bitcast(I32), 0)
-        nc.gpsimd.memset(xs[:, T // 2:T].bitcast(I32), 0)
-        gate_rows = keep.tile([P, P], F32, name="gate_rows")
-        nc.gpsimd.memset(gate_rows[:], 0.0)
-        w2s = keep.tile([P, N], U8, name="w2s", align_bytes=ALIGN)
-        nc.vector.memset(w2s[:].bitcast(I32), 0)
+        xs = placed.tile([P, T], U8, name="xs", align_bytes=ALIGN, offset=XS_AT)
+        nc.vector.memset(xs[QUADRANT:2 * QUADRANT, :].bitcast(I32), 0)
+        nc.vector.memset(xs[2 * QUADRANT:P, :].bitcast(I32), 0)
+        gs = keep.tile([P, S], U8, name="gs", align_bytes=ALIGN)
+        nc.gpsimd.memset(gs[:].bitcast(I32), 0)
         ident = keep.tile([P, P], F32, name="ident")
         make_identity(nc, ident[:])
+        minus_one = keep.tile([P, V], F32, name="minus_one")
+        nc.gpsimd.memset(minus_one[:], -1.0)
 
         def load_list(src, name):
             list_tile = keep.tile(list(src.shape), U16, name=name)
@@ -61,43 +70,50 @@ def tile_picked_lapl_none_p_kernel(tc, x_words, x_scales, w1, w2_words, w2_scale
             return list_tile
 
         def load_words(g):
-            table = keep.tile([P, T], I32, name="xw%d" % g, align_bytes=ALIGN)
+            table = placed.tile([P, T], I32, name="xw%d" % g, align_bytes=ALIGN, offset=WORDS_AT[g])
             nc.sync.dma_start(table[:], x_words[g].rearrange("p n t -> p (n t)").bitcast(I32))
             return table
 
+        raw_tiles = {}
+
         def load_w1(tile_no, g):
-            rows = keep.tile([P, PACK, P], F32, name="w1raw%d_%d" % (tile_no, g), tag="raw%d_%d" % (tile_no, g))
+            if tile_no == 0:
+                first = placed.tile([P, PACK, P], F32, name="w1first%d" % g, align_bytes=ALIGN, offset=FIRST_AT[g])
+                rows = first[:]
+            else:
+                if tile_no not in raw_tiles:
+                    raw_tiles[tile_no] = placed.tile([P, PASSES, PACK, P], F32, name="w1raw%d" % tile_no, align_bytes=ALIGN, offset=RAW_AT[tile_no])
+                rows = raw_tiles[tile_no][:, g, :, :]
             src = w1[g * K_PASS:(g + 1) * K_PASS, tile_no * P:(tile_no + 1) * P]
-            nc.sync.dma_start(rows[:], src.rearrange("(p t) c -> p t c", t=PACK))
-            return rows[:]
+            nc.sync.dma_start(rows, src.rearrange("(p t) c -> p t c", t=PACK))
+            return rows
 
         offs_t = load_list(offs, "offs_t")
-        cen_t = load_list(cen, "cen_t")
-        for q in range(QUADRANTS):
-            rows_q = xs[QUADRANT * q:QUADRANT * q + ROWS * PASSES, :]
-            nc.sync.dma_start(rows_q.bitcast(I32), x_scales[:, ROWS * q:ROWS * (q + 1), :].bitcast(I32))
+        for g in range(PASSES):
+            rows_g = xs[ROWS * QUADRANTS * g:ROWS * QUADRANTS * (g + 1), :]
+            nc.sync.dma_start(rows_g.bitcast(I32), x_scales[g].rearrange("(q j) n -> j q n", j=ROWS).bitcast(I32))
         xw = [load_words(0)]
-        nc.sync.dma_start(gate_rows[0:D * BLOCKS, :], gate[:, 0, :].rearrange("d (b n) -> d b n", n=P))
         raw = {(0, 0): load_w1(0, 0)}
-        xw.append(load_words(1))
-        raw[0, 1] = load_w1(0, 1)
+        cen_t = load_list(cen, "cen_t")
         neighbours = [load_list(src, name) for src, name in ((pos1, "pos1_t"), (pos2, "pos2_t"), (pos3, "pos3_t"))]
-        for tile_no in range(1, TILES):
-            for g in range(PASSES):
-                raw[tile_no, g] = load_w1(tile_no, g)
-        w2w = keep.tile([P, 2 * N], U8, name="w2w", align_bytes=ALIGN)
-        nc.sync.dma_start(w2w[:].bitcast(I32), w2_words[0].bitcast(I32))
-        for q in range(QUADRANTS):
-            rows_q = w2s[QUADRANT * q:QUADRANT * q + ROWS, :]
-            nc.sync.dma_start(rows_q.bitcast(I32), w2_scales[0, ROWS * q:ROWS * (q + 1), :].bitcast(I32))
+        xw.append(load_words(1))
 
         def round_w1(dst, src):
             nc.scalar.copy(dst.rearrange("p (c t) -> p c t", t=PACK), src.rearrange("p t c -> p c t"))
 
-        gs = keep.tile([P, S], U8, name="gs", align_bytes=ALIGN)
-        nc.vector.tensor_copy(gs[:], xs[:].indirect(offs_t[:]))
+        picked_rows = placed.tile([P, S], U8, name="picked_rows", align_bytes=ALIGN, offset=PICKED_AT)
+        nc.vector.tensor_copy(picked_rows[:], xs[:].indirect(offs_t[:]))
+        for q in range(QUADRANTS):
+            rows_q = gs[QUADRANT * q:QUADRANT * q + ROWS * PASSES, :]
+            nc.sync.dma_start(rows_q.bitcast(I32), picked_rows[q:QUADRANT:QUADRANTS, :].bitcast(I32))
+        for tile_no, g in ((0, 1), (1, 0), (1, 1)):
+            raw[tile_no, g] = load_w1(tile_no, g)
+        gates = placed.tile([P, D, V], F32, name="gates", align_bytes=ALIGN, offset=GATES_AT)
+        nc.sync.dma_start(gates[:], gate.rearrange("d p v -> p d v"))
         gw0 = keep.tile([P, S], U32, name="gw0", align_bytes=ALIGN)
         nc.vector.tensor_copy(gw0[:], xw[0][:].bitcast(U32).indirect(offs_t[:]))
+        for tile_no, g in ((2, 0), (2, 1)):
+            raw[tile_no, g] = load_w1(tile_no, g)
         picked = {(0, a): gw0[:, a:b] for a, b in PIECES}
 
         def pick_second_pass(a, b, tag):
@@ -116,24 +132,19 @@ def tile_picked_lapl_none_p_kernel(tc, x_words, x_scales, w1, w2_words, w2_scale
 
         quantise_first_tile(0)
 
-        turned = bank("zt3", [P, P], "turned")
-        nc.tensor.transpose(turned[:], gate_rows[:], ident[:])
-        gate_cols = keep.tile([P, D * BLOCKS], F32, name="gate_cols")
-        nc.scalar.activation(gate_cols[:], turned[:, 0:D * BLOCKS], COPY, scale=-1.0)
-        minus_gates = []
-        for d in range(D):
-            spread = bank("zt%d" % d, [P, V], "spread%d" % d)
-            for blk in range(BLOCKS):
-                col = d * BLOCKS + blk
-                nc.tensor.transpose(spread[:, blk * P:(blk + 1) * P], gate_cols[:, col:col + 1].to_broadcast([P, P]), ident[:])
-            minus_gate = keep.tile([P, V], F32, name="minus_gate%d" % d)
-            nc.scalar.copy(minus_gate[:], spread[:])
-            minus_gates.append(minus_gate)
-
         for a, b in PIECES[:-1]:
             pick_second_pass(a, b, "gw1_%d" % a)
         quantise_first_tile(1)
         pick_second_pass(PIECES[-1][0], PIECES[-1][1], "first1")
+        for g in range(PASSES):
+            raw[3, g] = load_w1(3, g)
+        w2w = placed.tile([P, 2 * N], U8, name="w2w", align_bytes=ALIGN, offset=W2_AT)
+        nc.sync.dma_start(w2w[:].bitcast(I32), w2_words[0].bitcast(I32))
+        w2s = placed.tile([P, N], U8, name="w2s", align_bytes=ALIGN, offset=W2_AT + 2 * N)
+        nc.vector.memset(w2s[:].bitcast(I32), 0)
+        for q in range(QUADRANTS):
+            rows_q = w2s[QUADRANT * q:QUADRANT * q + ROWS, :]
+            nc.sync.dma_start(rows_q.bitcast(I32), w2_scales[0, ROWS * q:ROWS * (q + 1), :].bitcast(I32))
 
         def mx_pass(acc, codes, scales, g, a, b):
             nc.tensor.matmul_mx(
@@ -167,7 +178,7 @@ def tile_picked_lapl_none_p_kernel(tc, x_words, x_scales, w1, w2_words, w2_scale
             codes = keep.tile([P, PASSES * P], U32, name="codes%d" % tile_no, align_bytes=ALIGN)
             scales = keep.tile([P, PASSES * P], U8, name="scales%d" % tile_no, align_bytes=ALIGN)
             nc.vector.quantize_mx(out=codes[:].bitcast(FP8X4), scales=scales[:], in_=rounded[:])
-            h_tile = keep.tile([P, S], F32, name="h%d" % tile_no, tag="raw%d_1" % (tile_no + 1))
+            h_tile = placed.tile([P, S], F32, name="h%d" % tile_no, align_bytes=ALIGN, offset=RAW_AT[tile_no + 1])
             tags = ("h3", "h0") if tile_no % 2 else ("h1", "h2")
             for half in range(S // BANK):
                 acc = bank(tags[half], [P, BANK], "acc%d_%d" % (tile_no, half))
@@ -201,7 +212,7 @@ def tile_picked_lapl_none_p_kernel(tc, x_words, x_scales, w1, w2_words, w2_scale
             centre = keep.tile([P, V], F32, name="centre%d" % tile_no)
             runs = RUNS if last else ((0, BLOCKS),)
             c0, c1 = runs[0][0] * P, runs[0][1] * P
-            nc.vector.tensor_copy(centre[:, c0:c1], h[:].indirect(entries(cen_t, c0, c1)))
+            nc.vector.tensor_tensor(centre[:, c0:c1], h[:].indirect(entries(cen_t, c0, c1)), minus_one[:, c0:c1], MULT)
             if tile_no == 0:
                 h_next = project(1, rounded_tiles[1])
             terms_tag = "rounded1" if tile_no == 0 else "terms%d" % tile_no
@@ -209,7 +220,7 @@ def tile_picked_lapl_none_p_kernel(tc, x_words, x_scales, w1, w2_words, w2_scale
             for run, (b0, b1) in enumerate(runs):
                 c0, c1 = b0 * P, b1 * P
                 if run > 0:
-                    nc.vector.tensor_copy(centre[:, c0:c1], h[:].indirect(entries(cen_t, c0, c1)))
+                    nc.vector.tensor_tensor(centre[:, c0:c1], h[:].indirect(entries(cen_t, c0, c1)), minus_one[:, c0:c1], MULT)
                 sums = [bank("zt%d" % blk, [P, P], "sum%d_%d" % (tile_no, blk)) for blk in range(b0, b1)]
                 for blk in range(b0, b1):
                     add_turned(sums[blk - b0][:], centre[:, blk * P:(blk + 1) * P], True, False)
@@ -218,12 +229,12 @@ def tile_picked_lapl_none_p_kernel(tc, x_words, x_scales, w1, w2_words, w2_scale
                     if last and b1 == BLOCKS and d == D - 1:
                         closing = keep.tile([P, c1 - c0], F32, name="closing", tag="zb0", align_bytes=ALIGN)
                         term = closing[:]
-                    nc.vector.tensor_tensor(term, h[:].indirect(entries(neighbours[d], c0, c1)), minus_gates[d][:, c0:c1], MULT)
+                    nc.vector.tensor_tensor(term, h[:].indirect(entries(neighbours[d], c0, c1)), gates[:, d, c0:c1], MULT)
                     for n in range(b1 - b0):
                         add_turned(sums[n][:], term[:, n * P:(n + 1) * P], False, d == D - 1)
                 span = slice(P // PACK * tile_no, P // PACK * (tile_no + 1))
                 for blk in range(b0, b1):
-                    nc.scalar.copy(zb[blk][:, :, span, :], sums[blk - b0][:].rearrange("v (r u e) -> v u r e", u=2, e=2))
+                    nc.scalar.activation(zb[blk][:, :, span, :], sums[blk - b0][:].rearrange("v (r u e) -> v u r e", u=2, e=2), COPY, scale=-1.0)
                 if last:
                     backs.append(turn_back(run, b0, b1))
             if not last:

@@ -31,14 +31,15 @@ BANK = 512
 ALIGN = 64
 PIECES = ((0, 512), (512, 768), (768, 1024))
 RUNS = ((0, 2), (2, 3), (3, 4))
+H_BANKS = 4
 KIB = 1024
 WORDS_AT = (0, 8 * KIB)
 XS_AT = 35 * KIB
-FIRST_AT = (16 * KIB, 34 * KIB)
-GATES_AT = 18 * KIB
-RAW_AT = (None, 36 * KIB, 24 * KIB, 8 * KIB, 28 * KIB)
-PICKED_AT = 24 * KIB - S // 2
+FIRST_AT = (16 * KIB, 18 * KIB)
+GATES_AT = (34 * KIB, 0, 12 * KIB)
+RAW_AT = (None, 36 * KIB, 2 * KIB, 8 * KIB, 28 * KIB)
 W2_AT = 14 * KIB
+ZB_AT = (44 * KIB, 45 * KIB, 46 * KIB, 47 * KIB)
 
 
 def tile_picked_lapl_none_p_kernel(tc, x_words, x_scales, w1, w2_words, w2_scales, gate, offs, cen, pos1, pos2, pos3, out):
@@ -74,6 +75,11 @@ def tile_picked_lapl_none_p_kernel(tc, x_words, x_scales, w1, w2_words, w2_scale
             nc.sync.dma_start(table[:], x_words[g].rearrange("p n t -> p (n t)").bitcast(I32))
             return table
 
+        def load_gate(d):
+            weights = placed.tile([P, V], F32, name="gate%d" % d, align_bytes=ALIGN, offset=GATES_AT[d])
+            nc.sync.dma_start(weights[:], gate[d])
+            return weights
+
         raw_tiles = {}
 
         def load_w1(tile_no, g):
@@ -95,23 +101,25 @@ def tile_picked_lapl_none_p_kernel(tc, x_words, x_scales, w1, w2_words, w2_scale
         xw = [load_words(0)]
         raw = {(0, 0): load_w1(0, 0)}
         cen_t = load_list(cen, "cen_t")
-        neighbours = [load_list(src, name) for src, name in ((pos1, "pos1_t"), (pos2, "pos2_t"), (pos3, "pos3_t"))]
+        neighbours = [load_list(pos1, "pos1_t")]
         xw.append(load_words(1))
+        raw[0, 1] = load_w1(0, 1)
+        neighbours.extend([load_list(pos2, "pos2_t"), load_list(pos3, "pos3_t")])
 
         def round_w1(dst, src):
             nc.scalar.copy(dst.rearrange("p (c t) -> p c t", t=PACK), src.rearrange("p t c -> p c t"))
 
-        picked_rows = placed.tile([P, S], U8, name="picked_rows", align_bytes=ALIGN, offset=PICKED_AT)
+        picked_rows = keep.tile([P, S], U8, name="picked_rows", align_bytes=ALIGN)
         nc.vector.tensor_copy(picked_rows[:], xs[:].indirect(offs_t[:]))
         for q in range(QUADRANTS):
             rows_q = gs[QUADRANT * q:QUADRANT * q + ROWS * PASSES, :]
             nc.sync.dma_start(rows_q.bitcast(I32), picked_rows[q:QUADRANT:QUADRANTS, :].bitcast(I32))
-        for tile_no, g in ((0, 1), (1, 0), (1, 1)):
-            raw[tile_no, g] = load_w1(tile_no, g)
-        gates = placed.tile([P, D, V], F32, name="gates", align_bytes=ALIGN, offset=GATES_AT)
-        nc.sync.dma_start(gates[:], gate.rearrange("d p v -> p d v"))
+        for g in range(PASSES):
+            raw[1, g] = load_w1(1, g)
+        gates = [load_gate(0)]
         gw0 = keep.tile([P, S], U32, name="gw0", align_bytes=ALIGN)
         nc.vector.tensor_copy(gw0[:], xw[0][:].bitcast(U32).indirect(offs_t[:]))
+        gates.append(load_gate(1))
         for tile_no, g in ((2, 0), (2, 1)):
             raw[tile_no, g] = load_w1(tile_no, g)
         picked = {(0, a): gw0[:, a:b] for a, b in PIECES}
@@ -121,21 +129,22 @@ def tile_picked_lapl_none_p_kernel(tc, x_words, x_scales, w1, w2_words, w2_scale
             nc.vector.tensor_copy(words[:], xw[1][:].bitcast(U32).indirect(entries(offs_t, a, b)))
             picked[1, a] = words[:]
 
-        codes0 = keep.tile([P, PASSES * P], U32, name="codes0", align_bytes=ALIGN)
+        codes0 = keep.tile([P, PASSES * P], U32, name="codes0", tag="codes0", align_bytes=ALIGN)
         scales0 = keep.tile([P, PASSES * P], U8, name="scales0", align_bytes=ALIGN)
 
-        def quantise_first_tile(g):
-            rounded = keep.tile([P, K_PASS], BF16, name="rounded0_%d" % g, tag="first%d" % g, align_bytes=ALIGN)
-            round_w1(rounded[:], raw[0, g])
+        def quantise_half(tile_no, g, codes, scales, tag):
+            rounded = keep.tile([P, K_PASS], BF16, name="rounded%d_%d" % (tile_no, g), tag=tag, align_bytes=ALIGN)
+            round_w1(rounded[:], raw[tile_no, g])
             cols = slice(g * P, (g + 1) * P)
-            nc.vector.quantize_mx(out=codes0[:, cols].bitcast(FP8X4), scales=scales0[:, cols], in_=rounded[:])
+            nc.vector.quantize_mx(out=codes[:, cols].bitcast(FP8X4), scales=scales[:, cols], in_=rounded[:])
 
-        quantise_first_tile(0)
+        quantise_half(0, 0, codes0, scales0, "first0")
 
         for a, b in PIECES[:-1]:
             pick_second_pass(a, b, "gw1_%d" % a)
-        quantise_first_tile(1)
+        quantise_half(0, 1, codes0, scales0, "first1")
         pick_second_pass(PIECES[-1][0], PIECES[-1][1], "first1")
+        gates.append(load_gate(2))
         for g in range(PASSES):
             raw[3, g] = load_w1(3, g)
         w2w = placed.tile([P, 2 * N], U8, name="w2w", align_bytes=ALIGN, offset=W2_AT)
@@ -174,22 +183,26 @@ def tile_picked_lapl_none_p_kernel(tc, x_words, x_scales, w1, w2_words, w2_scale
                 round_w1(rounded[:, g * K_PASS:(g + 1) * K_PASS], raw[tile_no, g])
             return rounded
 
+        codes1 = placed.tile([P, PASSES * P], U32, name="codes1", align_bytes=ALIGN, offset=ZB_AT[1] - KIB // 2)
+        scales1 = placed.tile([P, PASSES * P], U8, name="scales1", align_bytes=ALIGN, offset=ZB_AT[3] - P)
+        quantise_half(1, 0, codes1, scales1, "second0")
+
         def project(tile_no, rounded):
             codes = keep.tile([P, PASSES * P], U32, name="codes%d" % tile_no, align_bytes=ALIGN)
             scales = keep.tile([P, PASSES * P], U8, name="scales%d" % tile_no, align_bytes=ALIGN)
             nc.vector.quantize_mx(out=codes[:].bitcast(FP8X4), scales=scales[:], in_=rounded[:])
+            return products(tile_no, codes, scales)
+
+        def products(tile_no, codes, scales):
             h_tile = placed.tile([P, S], F32, name="h%d" % tile_no, align_bytes=ALIGN, offset=RAW_AT[tile_no + 1])
-            tags = ("h3", "h0") if tile_no % 2 else ("h1", "h2")
-            for half in range(S // BANK):
-                acc = bank(tags[half], [P, BANK], "acc%d_%d" % (tile_no, half))
-                for a, b in PIECES:
-                    if a // BANK == half:
-                        for g in range(PASSES):
-                            mx_pass(acc[:, a - BANK * half:b - BANK * half], codes, scales, g, a, b)
-                nc.scalar.copy(h_tile[:, BANK * half:BANK * (half + 1)], acc[:])
+            accs = [bank("h%d" % ((len(PIECES) * tile_no + n) % H_BANKS), [P, b - a], "acc%d_%d" % (tile_no, a)) for n, (a, b) in enumerate(PIECES)]
+            for g in range(PASSES):
+                for acc, (a, b) in zip(accs, PIECES):
+                    mx_pass(acc[:], codes, scales, g, a, b)
+            for acc, (a, b) in zip(accs, PIECES):
+                nc.scalar.copy(h_tile[:, a:b], acc[:])
             return h_tile
 
-        zb = [keep.tile([P, 2, P, 2], BF16, name="zb%d" % blk, tag="zb%d" % blk, align_bytes=ALIGN) for blk in range(BLOCKS)]
         result = keep.tile([P, V], F32, name="result")
 
         def turn_back(run, b0, b1):
@@ -204,7 +217,7 @@ def tile_picked_lapl_none_p_kernel(tc, x_words, x_scales, w1, w2_words, w2_scale
             nc.tensor.matmul(total, term, ident[:], start=start, stop=stop, is_transpose=True)
 
         backs = []
-        rounded_tiles = {tile_no: round_tile(tile_no) for tile_no in range(1, TILES)}
+        rounded_tiles = {2: round_tile(2)}
         for tile_no in range(TILES):
             last = tile_no == TILES - 1
             if 0 < tile_no < TILES - 1:
@@ -214,9 +227,13 @@ def tile_picked_lapl_none_p_kernel(tc, x_words, x_scales, w1, w2_words, w2_scale
             c0, c1 = runs[0][0] * P, runs[0][1] * P
             nc.vector.tensor_tensor(centre[:, c0:c1], h[:].indirect(entries(cen_t, c0, c1)), minus_one[:, c0:c1], MULT)
             if tile_no == 0:
-                h_next = project(1, rounded_tiles[1])
-            terms_tag = "rounded1" if tile_no == 0 else "terms%d" % tile_no
-            terms = keep.tile([P, D, V], F32, name="terms%d" % tile_no, tag=terms_tag, align_bytes=ALIGN)
+                quantise_half(1, 1, codes1, scales1, "codes0")
+                h_next = products(1, codes1, scales1)
+                rounded_tiles[3] = round_tile(3)
+                zb = [placed.tile([P, 2, P, 2], BF16, name="zb%d" % blk, align_bytes=ALIGN, offset=ZB_AT[blk]) for blk in range(BLOCKS)]
+                terms = placed.tile([P, D, V], F32, name="terms0", align_bytes=ALIGN, offset=RAW_AT[1])
+            else:
+                terms = keep.tile([P, D, V], F32, name="terms%d" % tile_no, align_bytes=ALIGN)
             for run, (b0, b1) in enumerate(runs):
                 c0, c1 = b0 * P, b1 * P
                 if run > 0:
@@ -227,9 +244,9 @@ def tile_picked_lapl_none_p_kernel(tc, x_words, x_scales, w1, w2_words, w2_scale
                 for d in range(D):
                     term = terms[:, d, c0:c1]
                     if last and b1 == BLOCKS and d == D - 1:
-                        closing = keep.tile([P, c1 - c0], F32, name="closing", tag="zb0", align_bytes=ALIGN)
+                        closing = placed.tile([P, c1 - c0], F32, name="closing", align_bytes=ALIGN, offset=ZB_AT[0])
                         term = closing[:]
-                    nc.vector.tensor_tensor(term, h[:].indirect(entries(neighbours[d], c0, c1)), gates[:, d, c0:c1], MULT)
+                    nc.vector.tensor_tensor(term, h[:].indirect(entries(neighbours[d], c0, c1)), gates[d][:, c0:c1], MULT)
                     for n in range(b1 - b0):
                         add_turned(sums[n][:], term[:, n * P:(n + 1) * P], False, d == D - 1)
                 span = slice(P // PACK * tile_no, P // PACK * (tile_no + 1))

@@ -31,6 +31,7 @@ BANK = 512
 ALIGN = 64
 PIECES = ((0, 512), (512, 768), (768, 1024))
 RUNS = ((0, 2), (2, 3), (3, 4))
+WARM_UPS = 4
 H_BANKS = 4
 KIB = 1024
 WORDS_AT = (0, 8 * KIB)
@@ -39,6 +40,7 @@ FIRST_AT = (16 * KIB, 18 * KIB)
 GATES_AT = (34 * KIB, 0, 12 * KIB)
 RAW_AT = (None, 36 * KIB, 2 * KIB, 8 * KIB, 28 * KIB)
 W2_AT = 14 * KIB
+SECOND_AT = 20 * KIB
 ZB_AT = (44 * KIB, 45 * KIB, 46 * KIB, 47 * KIB)
 
 
@@ -94,10 +96,10 @@ def tile_picked_lapl_none_p_kernel(tc, x_words, x_scales, w1, w2_words, w2_scale
             nc.sync.dma_start(rows, src.rearrange("(p t) c -> p t c", t=PACK))
             return rows
 
-        offs_t = load_list(offs, "offs_t")
         for g in range(PASSES):
             rows_g = xs[ROWS * QUADRANTS * g:ROWS * QUADRANTS * (g + 1), :]
             nc.sync.dma_start(rows_g.bitcast(I32), x_scales[g].rearrange("(q j) n -> j q n", j=ROWS).bitcast(I32))
+        offs_t = load_list(offs, "offs_t")
         xw = [load_words(0)]
         raw = {(0, 0): load_w1(0, 0)}
         cen_t = load_list(cen, "cen_t")
@@ -117,15 +119,30 @@ def tile_picked_lapl_none_p_kernel(tc, x_words, x_scales, w1, w2_words, w2_scale
         for g in range(PASSES):
             raw[1, g] = load_w1(1, g)
         gates = [load_gate(0)]
-        gw0 = keep.tile([P, S], U32, name="gw0", align_bytes=ALIGN)
-        nc.vector.tensor_copy(gw0[:], xw[0][:].bitcast(U32).indirect(offs_t[:]))
+        gw0 = []
+        for half in range(S // BANK):
+            words = keep.tile([P, BANK], U32, name="gw0_%d" % half, align_bytes=ALIGN)
+            nc.vector.tensor_copy(words[:], xw[0][:].bitcast(U32).indirect(entries(offs_t, half * BANK, (half + 1) * BANK)))
+            gw0.append(words)
+
+        idle = bank("zt0", [P, BANK], "idle")
+        for n in range(WARM_UPS):
+            nc.tensor.matmul_mx(
+                out=idle[:],
+                lhsT=gw0[0][:, 0:P].bitcast(FP8X4),
+                lhsT_scale=picked_rows[:, 0:P],
+                rhs=gw0[0][:].bitcast(FP8X4),
+                rhs_scale=picked_rows[:, 0:BANK],
+                start=True,
+                stop=True,
+            )
         gates.append(load_gate(1))
         for tile_no, g in ((2, 0), (2, 1)):
             raw[tile_no, g] = load_w1(tile_no, g)
-        picked = {(0, a): gw0[:, a:b] for a, b in PIECES}
+        picked = {(0, a): gw0[a // BANK][:, a % BANK:a % BANK + b - a] for a, b in PIECES}
 
-        def pick_second_pass(a, b, tag):
-            words = keep.tile([P, b - a], U32, name="gw1_%d" % a, tag=tag, align_bytes=ALIGN)
+        def pick_second_pass(a, b, at):
+            words = placed.tile([P, b - a], U32, name="gw1_%d" % a, align_bytes=ALIGN, offset=at)
             nc.vector.tensor_copy(words[:], xw[1][:].bitcast(U32).indirect(entries(offs_t, a, b)))
             picked[1, a] = words[:]
 
@@ -141,9 +158,9 @@ def tile_picked_lapl_none_p_kernel(tc, x_words, x_scales, w1, w2_words, w2_scale
         quantise_half(0, 0, codes0, scales0, "first0")
 
         for a, b in PIECES[:-1]:
-            pick_second_pass(a, b, "gw1_%d" % a)
+            pick_second_pass(a, b, SECOND_AT + PACK * a)
         quantise_half(0, 1, codes0, scales0, "first1")
-        pick_second_pass(PIECES[-1][0], PIECES[-1][1], "first1")
+        pick_second_pass(PIECES[-1][0], PIECES[-1][1], FIRST_AT[1])
         gates.append(load_gate(2))
         for g in range(PASSES):
             raw[3, g] = load_w1(3, g)
@@ -252,8 +269,8 @@ def tile_picked_lapl_none_p_kernel(tc, x_words, x_scales, w1, w2_words, w2_scale
                 span = slice(P // PACK * tile_no, P // PACK * (tile_no + 1))
                 for blk in range(b0, b1):
                     nc.scalar.activation(zb[blk][:, :, span, :], sums[blk - b0][:].rearrange("v (r u e) -> v u r e", u=2, e=2), COPY, scale=-1.0)
-                if last:
-                    backs.append(turn_back(run, b0, b1))
+                if last and run != 1:
+                    backs.extend(turn_back(r, RUNS[r][0], RUNS[r][1]) for r in range(len(backs), run + 1))
             if not last:
                 h = h_next
 
@@ -286,4 +303,4 @@ def tile_picked_lapl_none_p_kernel(tc, x_words, x_scales, w1, w2_words, w2_scale
                 nc.scalar.copy(result[:, 0:early], out_early[:])
                 nc.sync.dma_start(out[:, 0:early], result[:, 0:early])
         nc.vector.tensor_copy(result[:, early:V], out_last[:])
-        nc.scalar.dma_start(out[:, early:V], result[:, early:V])
+        nc.sync.dma_start(out[:, early:V], result[:, early:V])

@@ -31,7 +31,6 @@ BANK = 512
 ALIGN = 64
 PIECES = ((0, 512), (512, 768), (768, 1024))
 RUNS = ((0, 2), (2, 3), (3, 4))
-WARM_UPS = 4
 H_BANKS = 4
 KIB = 1024
 WORDS_AT = (0, 8 * KIB)
@@ -119,27 +118,12 @@ def tile_picked_lapl_none_p_kernel(tc, x_words, x_scales, w1, w2_words, w2_scale
         for g in range(PASSES):
             raw[1, g] = load_w1(1, g)
         gates = [load_gate(0)]
-        gw0 = []
-        for half in range(S // BANK):
-            words = keep.tile([P, BANK], U32, name="gw0_%d" % half, align_bytes=ALIGN)
-            nc.vector.tensor_copy(words[:], xw[0][:].bitcast(U32).indirect(entries(offs_t, half * BANK, (half + 1) * BANK)))
-            gw0.append(words)
-
-        idle = bank("zt0", [P, BANK], "idle")
-        for n in range(WARM_UPS):
-            nc.tensor.matmul_mx(
-                out=idle[:],
-                lhsT=gw0[0][:, 0:P].bitcast(FP8X4),
-                lhsT_scale=picked_rows[:, 0:P],
-                rhs=gw0[0][:].bitcast(FP8X4),
-                rhs_scale=picked_rows[:, 0:BANK],
-                start=True,
-                stop=True,
-            )
+        gw0 = keep.tile([P, S], U32, name="gw0", align_bytes=ALIGN)
+        nc.vector.tensor_copy(gw0[:], xw[0][:].bitcast(U32).indirect(offs_t[:]))
         gates.append(load_gate(1))
         for tile_no, g in ((2, 0), (2, 1)):
             raw[tile_no, g] = load_w1(tile_no, g)
-        picked = {(0, a): gw0[a // BANK][:, a % BANK:a % BANK + b - a] for a, b in PIECES}
+        picked = {(0, a): gw0[:, a:b] for a, b in PIECES}
 
         def pick_second_pass(a, b, at):
             words = placed.tile([P, b - a], U32, name="gw1_%d" % a, align_bytes=ALIGN, offset=at)
@@ -274,9 +258,6 @@ def tile_picked_lapl_none_p_kernel(tc, x_words, x_scales, w1, w2_words, w2_scale
             if not last:
                 h = h_next
 
-        early = RUNS[-1][0] * P
-        out_early = bank("h0", [P, early], "out_early")
-        out_last = bank("zt0", [P, V - early], "out_last")
         for run, (b0, b1) in enumerate(RUNS):
             closing_run = run == len(RUNS) - 1
             width = (b1 - b0) * P
@@ -290,8 +271,9 @@ def tile_picked_lapl_none_p_kernel(tc, x_words, x_scales, w1, w2_words, w2_scale
             z_codes = keep.tile([P, width], U32, name="z_codes%d" % run, align_bytes=ALIGN)
             z_scales = keep.tile([P, width], U8, name="z_scales%d" % run, align_bytes=ALIGN)
             nc.vector.quantize_mx(out=z_codes[:].bitcast(FP8X4), scales=z_scales[:], in_=zq[:])
+            product = bank("zt%d" % run, [P, width], "product%d" % run)
             nc.tensor.matmul_mx(
-                out=out_last[:] if closing_run else out_early[:, b0 * P:b1 * P],
+                out=product[:],
                 lhsT=w2w[:].bitcast(FP4X4),
                 lhsT_scale=w2s[:],
                 rhs=z_codes[:].bitcast(FP8X4),
@@ -299,8 +281,9 @@ def tile_picked_lapl_none_p_kernel(tc, x_words, x_scales, w1, w2_words, w2_scale
                 start=True,
                 stop=True,
             )
-            if b1 * P == early:
-                nc.scalar.copy(result[:, 0:early], out_early[:])
-                nc.sync.dma_start(out[:, 0:early], result[:, 0:early])
-        nc.vector.tensor_copy(result[:, early:V], out_last[:])
-        nc.sync.dma_start(out[:, early:V], result[:, early:V])
+            cols = slice(b0 * P, b1 * P)
+            if closing_run:
+                nc.vector.tensor_copy(result[:, cols], product[:])
+            else:
+                nc.scalar.copy(result[:, cols], product[:])
+            nc.sync.dma_start(out[:, cols], result[:, cols])

@@ -33,14 +33,19 @@ PIECES = ((0, 512), (512, 768), (768, 1024))
 RUNS = ((0, 2), (2, 3), (3, 4))
 H_BANKS = 4
 KIB = 1024
-WORDS_AT = (0, 8 * KIB)
+WORDS_AT = (8 * KIB, 0)
 XS_AT = 35 * KIB
-FIRST_AT = (16 * KIB, 18 * KIB)
-GATES_AT = (34 * KIB, 0, 12 * KIB)
-RAW_AT = (None, 36 * KIB, 2 * KIB, 8 * KIB, 28 * KIB)
-W2_AT = 14 * KIB
-SECOND_AT = 20 * KIB
-ZB_AT = (44 * KIB, 45 * KIB, 46 * KIB, 47 * KIB)
+FIRST_AT = (22 * KIB, 24 * KIB)
+GATES_AT = (34 * KIB, 8 * KIB, 10 * KIB)
+RAW_AT = (None, 36 * KIB, None, 0)
+HALVES_AT = {0: FIRST_AT, 2: (12 * KIB, 14 * KIB)}
+H_AT = (None, 48 * KIB, 0, 30 * KIB)
+CODES1_AT = 44 * KIB
+TERMS1_AT = 15 * KIB
+QUARTERS = ((0, 256), (256, 512), (512, 768), (768, 1024))
+W2_AT = 4 * KIB
+SECOND_AT = 26 * KIB
+ZB_AT = (52 * KIB, 53 * KIB, 54 * KIB, 55 * KIB)
 
 
 def tile_picked_lapl_none_p_kernel(tc, x_words, x_scales, w1, w2_words, w2_scales, gate, offs, cen, pos1, pos2, pos3, out):
@@ -84,8 +89,8 @@ def tile_picked_lapl_none_p_kernel(tc, x_words, x_scales, w1, w2_words, w2_scale
         raw_tiles = {}
 
         def load_w1(tile_no, g):
-            if tile_no == 0:
-                first = placed.tile([P, PACK, P], F32, name="w1first%d" % g, align_bytes=ALIGN, offset=FIRST_AT[g])
+            if tile_no in HALVES_AT:
+                first = placed.tile([P, PACK, P], F32, name="w1half%d_%d" % (tile_no, g), align_bytes=ALIGN, offset=HALVES_AT[tile_no][g])
                 rows = first[:]
             else:
                 if tile_no not in raw_tiles:
@@ -120,7 +125,7 @@ def tile_picked_lapl_none_p_kernel(tc, x_words, x_scales, w1, w2_words, w2_scale
         gates = [load_gate(0)]
         gw0 = keep.tile([P, S], U32, name="gw0", align_bytes=ALIGN)
         nc.vector.tensor_copy(gw0[:], xw[0][:].bitcast(U32).indirect(offs_t[:]))
-        gates.append(load_gate(1))
+        gates.extend([load_gate(1), load_gate(2)])
         for tile_no, g in ((2, 0), (2, 1)):
             raw[tile_no, g] = load_w1(tile_no, g)
         picked = {(0, a): gw0[:, a:b] for a, b in PIECES}
@@ -134,7 +139,10 @@ def tile_picked_lapl_none_p_kernel(tc, x_words, x_scales, w1, w2_words, w2_scale
         scales0 = keep.tile([P, PASSES * P], U8, name="scales0", align_bytes=ALIGN)
 
         def quantise_half(tile_no, g, codes, scales, tag):
-            rounded = keep.tile([P, K_PASS], BF16, name="rounded%d_%d" % (tile_no, g), tag=tag, align_bytes=ALIGN)
+            if tag is None:
+                rounded = placed.tile([P, K_PASS], BF16, name="rounded%d_%d" % (tile_no, g), align_bytes=ALIGN, offset=CODES1_AT)
+            else:
+                rounded = keep.tile([P, K_PASS], BF16, name="rounded%d_%d" % (tile_no, g), tag=tag, align_bytes=ALIGN)
             round_w1(rounded[:], raw[tile_no, g])
             cols = slice(g * P, (g + 1) * P)
             nc.vector.quantize_mx(out=codes[:, cols].bitcast(FP8X4), scales=scales[:, cols], in_=rounded[:])
@@ -145,7 +153,6 @@ def tile_picked_lapl_none_p_kernel(tc, x_words, x_scales, w1, w2_words, w2_scale
             pick_second_pass(a, b, SECOND_AT + PACK * a)
         quantise_half(0, 1, codes0, scales0, "first1")
         pick_second_pass(PIECES[-1][0], PIECES[-1][1], FIRST_AT[1])
-        gates.append(load_gate(2))
         for g in range(PASSES):
             raw[3, g] = load_w1(3, g)
         w2w = placed.tile([P, 2 * N], U8, name="w2w", align_bytes=ALIGN, offset=W2_AT)
@@ -156,19 +163,23 @@ def tile_picked_lapl_none_p_kernel(tc, x_words, x_scales, w1, w2_words, w2_scale
             rows_q = w2s[QUADRANT * q:QUADRANT * q + ROWS, :]
             nc.sync.dma_start(rows_q.bitcast(I32), w2_scales[0, ROWS * q:ROWS * (q + 1), :].bitcast(I32))
 
+        def picked_words(g, a, b):
+            first = max(lo for lo, hi in PIECES if lo <= a)
+            return picked[g, first][:, a - first:b - first]
+
         def mx_pass(acc, codes, scales, g, a, b):
             nc.tensor.matmul_mx(
                 out=acc,
                 lhsT=codes[:, g * P:(g + 1) * P].bitcast(FP8X4),
                 lhsT_scale=scales[:, g * P:(g + 1) * P],
-                rhs=picked[g, a].bitcast(FP8X4),
+                rhs=picked_words(g, a, b).bitcast(FP8X4),
                 rhs_scale=gs[ROWS * g:P, a:b],
                 start=(g == 0),
                 stop=(g == PASSES - 1),
             )
 
         h = keep.tile([P, S], F32, name="h0")
-        accs = [bank("h%d" % n, [P, b - a], "acc0_%d" % a) for n, (a, b) in enumerate(PIECES)]
+        accs = [bank("b%d" % n, [P, b - a], "acc0_%d" % a) for n, (a, b) in enumerate(PIECES)]
         for g in range(PASSES):
             for acc, (a, b) in zip(accs, PIECES):
                 mx_pass(acc[:], codes0, scales0, g, a, b)
@@ -184,8 +195,8 @@ def tile_picked_lapl_none_p_kernel(tc, x_words, x_scales, w1, w2_words, w2_scale
                 round_w1(rounded[:, g * K_PASS:(g + 1) * K_PASS], raw[tile_no, g])
             return rounded
 
-        codes1 = placed.tile([P, PASSES * P], U32, name="codes1", align_bytes=ALIGN, offset=ZB_AT[1] - KIB // 2)
-        scales1 = placed.tile([P, PASSES * P], U8, name="scales1", align_bytes=ALIGN, offset=ZB_AT[3] - P)
+        codes1 = placed.tile([P, PASSES * P], U32, name="codes1", align_bytes=ALIGN, offset=CODES1_AT)
+        scales1 = keep.tile([P, PASSES * P], U8, name="scales1", align_bytes=ALIGN)
         quantise_half(1, 0, codes1, scales1, "second0")
 
         def project(tile_no, rounded):
@@ -195,19 +206,19 @@ def tile_picked_lapl_none_p_kernel(tc, x_words, x_scales, w1, w2_words, w2_scale
             return products(tile_no, codes, scales)
 
         def products(tile_no, codes, scales):
-            h_tile = placed.tile([P, S], F32, name="h%d" % tile_no, align_bytes=ALIGN, offset=RAW_AT[tile_no + 1])
-            accs = [bank("h%d" % ((len(PIECES) * tile_no + n) % H_BANKS), [P, b - a], "acc%d_%d" % (tile_no, a)) for n, (a, b) in enumerate(PIECES)]
+            h_tile = placed.tile([P, S], F32, name="h%d" % tile_no, align_bytes=ALIGN, offset=H_AT[tile_no])
+            accs = [bank("b%d" % (H_BANKS * (tile_no % 2) + n), [P, b - a], "acc%d_%d" % (tile_no, a)) for n, (a, b) in enumerate(QUARTERS)]
             for g in range(PASSES):
-                for acc, (a, b) in zip(accs, PIECES):
+                for acc, (a, b) in zip(accs, QUARTERS):
                     mx_pass(acc[:], codes, scales, g, a, b)
-            for acc, (a, b) in zip(accs, PIECES):
+            for acc, (a, b) in zip(accs, QUARTERS):
                 nc.scalar.copy(h_tile[:, a:b], acc[:])
             return h_tile
 
         result = keep.tile([P, V], F32, name="result")
 
         def turn_back(run, b0, b1):
-            back = bank("h%d" % (run + 1), [P, b1 - b0, 2, P], "back%d" % run)
+            back = bank("b%d" % (H_BANKS + run + 1), [P, b1 - b0, 2, P], "back%d" % run)
             for blk in range(b0, b1):
                 pairs = zb[blk][:].rearrange("v u p e -> v (u p e)").bitcast(F32)
                 for u in range(2):
@@ -218,11 +229,15 @@ def tile_picked_lapl_none_p_kernel(tc, x_words, x_scales, w1, w2_words, w2_scale
             nc.tensor.matmul(total, term, ident[:], start=start, stop=stop, is_transpose=True)
 
         backs = []
-        rounded_tiles = {2: round_tile(2)}
+        rounded_tiles = {}
+        codes2 = keep.tile([P, PASSES * P], U32, name="codes2", align_bytes=ALIGN)
+        scales2 = keep.tile([P, PASSES * P], U8, name="scales2", align_bytes=ALIGN)
         for tile_no in range(TILES):
             last = tile_no == TILES - 1
-            if 0 < tile_no < TILES - 1:
-                h_next = project(tile_no + 1, rounded_tiles[tile_no + 1])
+            if tile_no == 1:
+                quantise_half(2, 0, codes2, scales2, "third0")
+            if tile_no == 2:
+                h_next = project(3, rounded_tiles[3])
             centre = keep.tile([P, V], F32, name="centre%d" % tile_no)
             runs = RUNS if last else ((0, BLOCKS),)
             c0, c1 = runs[0][0] * P, runs[0][1] * P
@@ -230,20 +245,27 @@ def tile_picked_lapl_none_p_kernel(tc, x_words, x_scales, w1, w2_words, w2_scale
             if tile_no == 0:
                 quantise_half(1, 1, codes1, scales1, "codes0")
                 h_next = products(1, codes1, scales1)
-                rounded_tiles[3] = round_tile(3)
                 zb = [placed.tile([P, 2, P, 2], BF16, name="zb%d" % blk, align_bytes=ALIGN, offset=ZB_AT[blk]) for blk in range(BLOCKS)]
-                terms = placed.tile([P, D, V], F32, name="terms0", align_bytes=ALIGN, offset=RAW_AT[1])
+                terms0 = placed.tile([P, D, V], F32, name="terms0", align_bytes=ALIGN, offset=RAW_AT[1])
+                terms = [terms0[:, d, :] for d in range(D)]
+            elif tile_no == 1:
+                quantise_half(2, 1, codes2, scales2, None)
+                rounded_tiles[3] = round_tile(3)
+                h_next = products(2, codes2, scales2)
+                terms1 = placed.tile([P, D, V], F32, name="terms1", align_bytes=ALIGN, offset=TERMS1_AT)
+                terms = [terms1[:, d, :] for d in range(D)]
             else:
-                terms = keep.tile([P, D, V], F32, name="terms%d" % tile_no, align_bytes=ALIGN)
+                terms_n = keep.tile([P, D, V], F32, name="terms%d" % tile_no, align_bytes=ALIGN)
+                terms = [terms_n[:, d, :] for d in range(D)]
             for run, (b0, b1) in enumerate(runs):
                 c0, c1 = b0 * P, b1 * P
                 if run > 0:
                     nc.vector.tensor_tensor(centre[:, c0:c1], h[:].indirect(entries(cen_t, c0, c1)), minus_one[:, c0:c1], MULT)
-                sums = [bank("zt%d" % blk, [P, P], "sum%d_%d" % (tile_no, blk)) for blk in range(b0, b1)]
+                sums = [bank("b%d" % (H_BANKS * ((tile_no + 1) % 2) + blk), [P, P], "sum%d_%d" % (tile_no, blk)) for blk in range(b0, b1)]
                 for blk in range(b0, b1):
                     add_turned(sums[blk - b0][:], centre[:, blk * P:(blk + 1) * P], True, False)
                 for d in range(D):
-                    term = terms[:, d, c0:c1]
+                    term = terms[d][:, c0:c1]
                     if last and b1 == BLOCKS and d == D - 1:
                         closing = placed.tile([P, c1 - c0], F32, name="closing", align_bytes=ALIGN, offset=ZB_AT[0])
                         term = closing[:]
@@ -271,7 +293,7 @@ def tile_picked_lapl_none_p_kernel(tc, x_words, x_scales, w1, w2_words, w2_scale
             z_codes = keep.tile([P, width], U32, name="z_codes%d" % run, align_bytes=ALIGN)
             z_scales = keep.tile([P, width], U8, name="z_scales%d" % run, align_bytes=ALIGN)
             nc.vector.quantize_mx(out=z_codes[:].bitcast(FP8X4), scales=z_scales[:], in_=zq[:])
-            product = bank("zt%d" % run, [P, width], "product%d" % run)
+            product = bank("b%d" % run, [P, width], "product%d" % run)
             nc.tensor.matmul_mx(
                 out=product[:],
                 lhsT=w2w[:].bitcast(FP4X4),

@@ -41,7 +41,7 @@ RAW_AT = (None, 36 * KIB, None, 0)
 HALVES_AT = {0: FIRST_AT, 2: (12 * KIB, 14 * KIB)}
 H_AT = (None, 48 * KIB, 0, 30 * KIB)
 CODES1_AT = 44 * KIB
-TERMS1_AT = 15 * KIB
+TERMS1_AT = 14 * KIB
 QUARTERS = ((0, 256), (256, 512), (512, 768), (768, 1024))
 W2_AT = 4 * KIB
 SECOND_AT = 26 * KIB
@@ -236,9 +236,16 @@ def tile_picked_lapl_none_p_kernel(tc, x_words, x_scales, w1, w2_words, w2_scale
             last = tile_no == TILES - 1
             if tile_no == 1:
                 quantise_half(2, 0, codes2, scales2, "third0")
+                quantise_half(2, 1, codes2, scales2, None)
+                rounded_tiles[3] = round_tile(3)
+                h_next = products(2, codes2, scales2)
             if tile_no == 2:
                 h_next = project(3, rounded_tiles[3])
-            centre = keep.tile([P, V], F32, name="centre%d" % tile_no)
+            if tile_no == 1:
+                four = placed.tile([P, D + 1, V], F32, name="terms1", align_bytes=ALIGN, offset=TERMS1_AT)
+                centre = four[:, D, :]
+            else:
+                centre = keep.tile([P, V], F32, name="centre%d" % tile_no)
             runs = RUNS if last else ((0, BLOCKS),)
             c0, c1 = runs[0][0] * P, runs[0][1] * P
             nc.vector.tensor_tensor(centre[:, c0:c1], h[:].indirect(entries(cen_t, c0, c1)), minus_one[:, c0:c1], MULT)
@@ -249,11 +256,7 @@ def tile_picked_lapl_none_p_kernel(tc, x_words, x_scales, w1, w2_words, w2_scale
                 terms0 = placed.tile([P, D, V], F32, name="terms0", align_bytes=ALIGN, offset=RAW_AT[1])
                 terms = [terms0[:, d, :] for d in range(D)]
             elif tile_no == 1:
-                quantise_half(2, 1, codes2, scales2, None)
-                rounded_tiles[3] = round_tile(3)
-                h_next = products(2, codes2, scales2)
-                terms1 = placed.tile([P, D, V], F32, name="terms1", align_bytes=ALIGN, offset=TERMS1_AT)
-                terms = [terms1[:, d, :] for d in range(D)]
+                terms = [four[:, d, :] for d in range(D)]
             else:
                 terms_n = keep.tile([P, D, V], F32, name="terms%d" % tile_no, align_bytes=ALIGN)
                 terms = [terms_n[:, d, :] for d in range(D)]

@@ -33,17 +33,17 @@ PIECES = ((0, 512), (512, 768), (768, 1024))
 RUNS = ((0, 2), (2, 3), (3, 4))
 H_BANKS = 4
 KIB = 1024
-WORDS_AT = (8 * KIB, 0)
+WORDS_AT = (8 * KIB, 60 * KIB)
 XS_AT = 35 * KIB
 FIRST_AT = (22 * KIB, 24 * KIB)
 GATES_AT = (34 * KIB, 8 * KIB, 10 * KIB)
-RAW_AT = (None, 36 * KIB, None, 0)
-HALVES_AT = {0: FIRST_AT, 2: (12 * KIB, 14 * KIB)}
+RAW_AT = (None, 36 * KIB)
+HALVES_AT = {0: FIRST_AT, 2: (12 * KIB, 14 * KIB), 3: (60 * KIB, 66 * KIB)}
 H_AT = (None, 48 * KIB, 0, 30 * KIB)
-CODES1_AT = 44 * KIB
+CODES_AT = (None, 44 * KIB, 46 * KIB)
 TERMS1_AT = 14 * KIB
 QUARTERS = ((0, 256), (256, 512), (512, 768), (768, 1024))
-W2_AT = 4 * KIB
+W2_AT = 62 * KIB
 SECOND_AT = 26 * KIB
 ZB_AT = (52 * KIB, 53 * KIB, 54 * KIB, 55 * KIB)
 
@@ -140,7 +140,7 @@ def tile_picked_lapl_none_p_kernel(tc, x_words, x_scales, w1, w2_words, w2_scale
 
         def quantise_half(tile_no, g, codes, scales, tag):
             if tag is None:
-                rounded = placed.tile([P, K_PASS], BF16, name="rounded%d_%d" % (tile_no, g), align_bytes=ALIGN, offset=CODES1_AT)
+                rounded = placed.tile([P, K_PASS], BF16, name="rounded%d_%d" % (tile_no, g), align_bytes=ALIGN, offset=CODES_AT[tile_no - 1])
             else:
                 rounded = keep.tile([P, K_PASS], BF16, name="rounded%d_%d" % (tile_no, g), tag=tag, align_bytes=ALIGN)
             round_w1(rounded[:], raw[tile_no, g])
@@ -189,21 +189,9 @@ def tile_picked_lapl_none_p_kernel(tc, x_words, x_scales, w1, w2_words, w2_scale
             else:
                 nc.vector.tensor_copy(h[:, a:b], acc[:])
 
-        def round_tile(tile_no):
-            rounded = keep.tile([P, PASSES * K_PASS], BF16, name="rounded%d" % tile_no, tag="rounded%d" % tile_no, align_bytes=ALIGN)
-            for g in range(PASSES):
-                round_w1(rounded[:, g * K_PASS:(g + 1) * K_PASS], raw[tile_no, g])
-            return rounded
-
-        codes1 = placed.tile([P, PASSES * P], U32, name="codes1", align_bytes=ALIGN, offset=CODES1_AT)
+        codes1 = placed.tile([P, PASSES * P], U32, name="codes1", align_bytes=ALIGN, offset=CODES_AT[1])
         scales1 = keep.tile([P, PASSES * P], U8, name="scales1", align_bytes=ALIGN)
         quantise_half(1, 0, codes1, scales1, "second0")
-
-        def project(tile_no, rounded):
-            codes = keep.tile([P, PASSES * P], U32, name="codes%d" % tile_no, align_bytes=ALIGN)
-            scales = keep.tile([P, PASSES * P], U8, name="scales%d" % tile_no, align_bytes=ALIGN)
-            nc.vector.quantize_mx(out=codes[:].bitcast(FP8X4), scales=scales[:], in_=rounded[:])
-            return products(tile_no, codes, scales)
 
         def products(tile_no, codes, scales):
             h_tile = placed.tile([P, S], F32, name="h%d" % tile_no, align_bytes=ALIGN, offset=H_AT[tile_no])
@@ -229,21 +217,23 @@ def tile_picked_lapl_none_p_kernel(tc, x_words, x_scales, w1, w2_words, w2_scale
             nc.tensor.matmul(total, term, ident[:], start=start, stop=stop, is_transpose=True)
 
         backs = []
-        rounded_tiles = {}
-        codes2 = keep.tile([P, PASSES * P], U32, name="codes2", align_bytes=ALIGN)
+        codes2 = placed.tile([P, PASSES * P], U32, name="codes2", align_bytes=ALIGN, offset=CODES_AT[2])
+        codes3 = keep.tile([P, PASSES * P], U32, name="codes3", align_bytes=ALIGN)
+        scales3 = keep.tile([P, PASSES * P], U8, name="scales3", align_bytes=ALIGN)
         scales2 = keep.tile([P, PASSES * P], U8, name="scales2", align_bytes=ALIGN)
         for tile_no in range(TILES):
             last = tile_no == TILES - 1
             if tile_no == 1:
                 quantise_half(2, 0, codes2, scales2, "third0")
                 quantise_half(2, 1, codes2, scales2, None)
-                rounded_tiles[3] = round_tile(3)
                 h_next = products(2, codes2, scales2)
             if tile_no == 2:
-                h_next = project(3, rounded_tiles[3])
+                quantise_half(3, 0, codes3, scales3, "fourth0")
             if tile_no == 1:
                 four = placed.tile([P, D + 1, V], F32, name="terms1", align_bytes=ALIGN, offset=TERMS1_AT)
                 centre = four[:, D, :]
+            elif tile_no == 2:
+                centre = placed.tile([P, V], F32, name="centre2", align_bytes=ALIGN, offset=HALVES_AT[3][0])
             else:
                 centre = keep.tile([P, V], F32, name="centre%d" % tile_no)
             runs = RUNS if last else ((0, BLOCKS),)
@@ -257,6 +247,11 @@ def tile_picked_lapl_none_p_kernel(tc, x_words, x_scales, w1, w2_words, w2_scale
                 terms = [terms0[:, d, :] for d in range(D)]
             elif tile_no == 1:
                 terms = [four[:, d, :] for d in range(D)]
+            elif tile_no == 2:
+                quantise_half(3, 1, codes3, scales3, None)
+                h_next = products(3, codes3, scales3)
+                terms2 = placed.tile([P, D, V], F32, name="terms2", align_bytes=ALIGN, offset=HALVES_AT[3][1])
+                terms = [terms2[:, d, :] for d in range(D)]
             else:
                 terms_n = keep.tile([P, D, V], F32, name="terms%d" % tile_no, align_bytes=ALIGN)
                 terms = [terms_n[:, d, :] for d in range(D)]

@@ -31,21 +31,23 @@ BANK = 512
 ALIGN = 64
 PIECES = ((0, 512), (512, 768), (768, 1024))
 RUNS = ((0, 2), (2, 3), (3, 4))
-H_BANKS = 4
 KIB = 1024
 WORDS_AT = (8 * KIB, 60 * KIB)
 XS_AT = 35 * KIB
-FIRST_AT = (22 * KIB, 24 * KIB)
-GATES_AT = (34 * KIB, 8 * KIB, 10 * KIB)
-RAW_AT = (None, 36 * KIB)
-HALVES_AT = {0: FIRST_AT, 2: (12 * KIB, 14 * KIB), 3: (60 * KIB, 66 * KIB)}
-H_AT = (None, 48 * KIB, 0, 30 * KIB)
-CODES_AT = (None, 44 * KIB, 46 * KIB)
-TERMS1_AT = 14 * KIB
-QUARTERS = ((0, 256), (256, 512), (512, 768), (768, 1024))
-W2_AT = 62 * KIB
+RAW_AT = {(0, 0): 22 * KIB, (0, 1): 24 * KIB, (2, 0): 8 * KIB, (2, 1): 14 * KIB, (3, 0): 60 * KIB, (3, 1): 66 * KIB}
+RAW1_AT = 36 * KIB
+GATES_AT = (34 * KIB, 10 * KIB, 12 * KIB)
 SECOND_AT = 26 * KIB
-ZB_AT = (52 * KIB, 53 * KIB, 54 * KIB, 55 * KIB)
+W2_AT = 62 * KIB
+LATER_AT = (38 * KIB, 14 * KIB, 66 * KIB)
+CODES_AT = (44 * KIB, 47 * KIB, 50 * KIB, 53 * KIB)
+ROUNDED_AT = {(1, 1): CODES_AT[0], (2, 1): CODES_AT[1] - KIB // 2, (3, 0): CODES_AT[1] + KIB // 2, (3, 1): CODES_AT[2]}
+ZB_AT = CODES_AT[3]
+PRODUCT_BANKS = ((0, 1, 2), (3, 1), (0, 2), (3, 1))
+SUM_BANKS = (4, 5, 6)
+RUN_SUM_BANKS = (7, 4, 7)
+BACK_BANKS = (0, 2, 3)
+RESULT_BANKS = (1, 5, 6)
 
 
 def tile_picked_lapl_none_p_kernel(tc, x_words, x_scales, w1, w2_words, w2_scales, gate, offs, cen, pos1, pos2, pos3, out):
@@ -55,21 +57,24 @@ def tile_picked_lapl_none_p_kernel(tc, x_words, x_scales, w1, w2_words, w2_scale
         psum = ctx.enter_context(tc.psum_pool(name="psum", bufs=1))
         placed = ctx.enter_context(tc.tile_pool(name="placed", bufs=1))
 
-        def bank(tag, shape, name):
-            return psum.tile(shape, F32, name=name, tag=tag)
+        def bank(number, shape, name):
+            return psum.tile(shape, F32, name=name, tag="b%d" % number)
+
+        def place(shape, dtype, name, at):
+            if at is None:
+                return keep.tile(shape, dtype, name=name, align_bytes=ALIGN)
+            return placed.tile(shape, dtype, name=name, align_bytes=ALIGN, offset=at)
 
         def entries(list_tile, a, b):
             return list_tile[:, a // PER_COLUMN:b // PER_COLUMN]
 
-        xs = placed.tile([P, T], U8, name="xs", align_bytes=ALIGN, offset=XS_AT)
+        xs = place([P, T], U8, "xs", XS_AT)
         nc.vector.memset(xs[QUADRANT:2 * QUADRANT, :].bitcast(I32), 0)
         nc.vector.memset(xs[2 * QUADRANT:P, :].bitcast(I32), 0)
-        gs = keep.tile([P, S], U8, name="gs", align_bytes=ALIGN)
+        gs = place([P, S], U8, "gs", None)
         nc.gpsimd.memset(gs[:].bitcast(I32), 0)
-        ident = keep.tile([P, P], F32, name="ident")
+        ident = place([P, P], F32, "ident", None)
         make_identity(nc, ident[:])
-        minus_one = keep.tile([P, V], F32, name="minus_one")
-        nc.gpsimd.memset(minus_one[:], -1.0)
 
         def load_list(src, name):
             list_tile = keep.tile(list(src.shape), U16, name=name)
@@ -77,221 +82,215 @@ def tile_picked_lapl_none_p_kernel(tc, x_words, x_scales, w1, w2_words, w2_scale
             return list_tile
 
         def load_words(g):
-            table = placed.tile([P, T], I32, name="xw%d" % g, align_bytes=ALIGN, offset=WORDS_AT[g])
+            table = place([P, T], I32, "xw%d" % g, WORDS_AT[g])
             nc.sync.dma_start(table[:], x_words[g].rearrange("p n t -> p (n t)").bitcast(I32))
             return table
 
         def load_gate(d):
-            weights = placed.tile([P, V], F32, name="gate%d" % d, align_bytes=ALIGN, offset=GATES_AT[d])
+            weights = place([P, V], F32, "gate%d" % d, GATES_AT[d])
             nc.sync.dma_start(weights[:], gate[d])
             return weights
 
-        raw_tiles = {}
+        raw = {}
 
-        def load_w1(tile_no, g):
-            if tile_no in HALVES_AT:
-                first = placed.tile([P, PACK, P], F32, name="w1half%d_%d" % (tile_no, g), align_bytes=ALIGN, offset=HALVES_AT[tile_no][g])
-                rows = first[:]
-            else:
-                if tile_no not in raw_tiles:
-                    raw_tiles[tile_no] = placed.tile([P, PASSES, PACK, P], F32, name="w1raw%d" % tile_no, align_bytes=ALIGN, offset=RAW_AT[tile_no])
-                rows = raw_tiles[tile_no][:, g, :, :]
+        def load_w1(tile_no, g, rows=None):
+            if rows is None:
+                rows = place([P, PACK, P], F32, "raw%d_%d" % (tile_no, g), RAW_AT[tile_no, g])[:]
             src = w1[g * K_PASS:(g + 1) * K_PASS, tile_no * P:(tile_no + 1) * P]
             nc.sync.dma_start(rows, src.rearrange("(p t) c -> p t c", t=PACK))
-            return rows
+            raw[tile_no, g] = rows
 
         for g in range(PASSES):
             rows_g = xs[ROWS * QUADRANTS * g:ROWS * QUADRANTS * (g + 1), :]
             nc.sync.dma_start(rows_g.bitcast(I32), x_scales[g].rearrange("(q j) n -> j q n", j=ROWS).bitcast(I32))
         offs_t = load_list(offs, "offs_t")
         xw = [load_words(0)]
-        raw = {(0, 0): load_w1(0, 0)}
+        load_w1(0, 0)
         cen_t = load_list(cen, "cen_t")
         neighbours = [load_list(pos1, "pos1_t")]
         xw.append(load_words(1))
-        raw[0, 1] = load_w1(0, 1)
+        load_w1(0, 1)
         neighbours.extend([load_list(pos2, "pos2_t"), load_list(pos3, "pos3_t")])
 
-        def round_w1(dst, src):
-            nc.scalar.copy(dst.rearrange("p (c t) -> p c t", t=PACK), src.rearrange("p t c -> p c t"))
-
-        picked_rows = keep.tile([P, S], U8, name="picked_rows", align_bytes=ALIGN)
+        picked_rows = place([P, S], U8, "picked_rows", None)
         nc.vector.tensor_copy(picked_rows[:], xs[:].indirect(offs_t[:]))
         for q in range(QUADRANTS):
             rows_q = gs[QUADRANT * q:QUADRANT * q + ROWS * PASSES, :]
             nc.sync.dma_start(rows_q.bitcast(I32), picked_rows[q:QUADRANT:QUADRANTS, :].bitcast(I32))
+        raw1 = place([P, PASSES, PACK, P], F32, "raw1", RAW1_AT)
         for g in range(PASSES):
-            raw[1, g] = load_w1(1, g)
+            load_w1(1, g, raw1[:, g, :, :])
         gates = [load_gate(0)]
-        gw0 = keep.tile([P, S], U32, name="gw0", align_bytes=ALIGN)
+        gw0 = place([P, S], U32, "gw0", None)
         nc.vector.tensor_copy(gw0[:], xw[0][:].bitcast(U32).indirect(offs_t[:]))
+        load_w1(2, 0)
         gates.extend([load_gate(1), load_gate(2)])
-        for tile_no, g in ((2, 0), (2, 1)):
-            raw[tile_no, g] = load_w1(tile_no, g)
+        load_w1(2, 1)
         picked = {(0, a): gw0[:, a:b] for a, b in PIECES}
 
         def pick_second_pass(a, b, at):
-            words = placed.tile([P, b - a], U32, name="gw1_%d" % a, align_bytes=ALIGN, offset=at)
+            words = place([P, b - a], U32, "gw1_%d" % a, at)
             nc.vector.tensor_copy(words[:], xw[1][:].bitcast(U32).indirect(entries(offs_t, a, b)))
             picked[1, a] = words[:]
 
-        codes0 = keep.tile([P, PASSES * P], U32, name="codes0", tag="codes0", align_bytes=ALIGN)
-        scales0 = keep.tile([P, PASSES * P], U8, name="scales0", align_bytes=ALIGN)
+        codes = {}
+        scales = {}
+        rounded = {}
 
-        def quantise_half(tile_no, g, codes, scales, tag):
-            if tag is None:
-                rounded = placed.tile([P, K_PASS], BF16, name="rounded%d_%d" % (tile_no, g), align_bytes=ALIGN, offset=CODES_AT[tile_no - 1])
-            else:
-                rounded = keep.tile([P, K_PASS], BF16, name="rounded%d_%d" % (tile_no, g), tag=tag, align_bytes=ALIGN)
-            round_w1(rounded[:], raw[tile_no, g])
+        def round_half(tile_no, g):
+            rounded[tile_no, g] = place([P, K_PASS], BF16, "rounded%d_%d" % (tile_no, g), ROUNDED_AT.get((tile_no, g)))
+            nc.scalar.copy(rounded[tile_no, g][:].rearrange("p (c t) -> p c t", t=PACK), raw[tile_no, g].rearrange("p t c -> p c t"))
+
+        def quantise_half(tile_no, g):
+            if g == 0:
+                codes[tile_no] = place([P, PASSES * P], U32, "codes%d" % tile_no, CODES_AT[tile_no])
+                scales[tile_no] = place([P, PASSES * P], U8, "scales%d" % tile_no, None)
             cols = slice(g * P, (g + 1) * P)
-            nc.vector.quantize_mx(out=codes[:, cols].bitcast(FP8X4), scales=scales[:, cols], in_=rounded[:])
+            nc.vector.quantize_mx(out=codes[tile_no][:, cols].bitcast(FP8X4), scales=scales[tile_no][:, cols], in_=rounded[tile_no, g][:])
 
-        quantise_half(0, 0, codes0, scales0, "first0")
-
+        round_half(0, 0)
+        quantise_half(0, 0)
         for a, b in PIECES[:-1]:
             pick_second_pass(a, b, SECOND_AT + PACK * a)
-        quantise_half(0, 1, codes0, scales0, "first1")
-        pick_second_pass(PIECES[-1][0], PIECES[-1][1], FIRST_AT[1])
+        round_half(0, 1)
+        quantise_half(0, 1)
+        pick_second_pass(PIECES[-1][0], PIECES[-1][1], RAW_AT[0, 1])
         for g in range(PASSES):
-            raw[3, g] = load_w1(3, g)
-        w2w = placed.tile([P, 2 * N], U8, name="w2w", align_bytes=ALIGN, offset=W2_AT)
+            load_w1(3, g)
+        w2w = place([P, 2 * N], U8, "w2w", W2_AT)
         nc.sync.dma_start(w2w[:].bitcast(I32), w2_words[0].bitcast(I32))
-        w2s = placed.tile([P, N], U8, name="w2s", align_bytes=ALIGN, offset=W2_AT + 2 * N)
+        w2s = place([P, N], U8, "w2s", W2_AT + 2 * N)
         nc.vector.memset(w2s[:].bitcast(I32), 0)
         for q in range(QUADRANTS):
             rows_q = w2s[QUADRANT * q:QUADRANT * q + ROWS, :]
             nc.sync.dma_start(rows_q.bitcast(I32), w2_scales[0, ROWS * q:ROWS * (q + 1), :].bitcast(I32))
 
-        def picked_words(g, a, b):
-            first = max(lo for lo, hi in PIECES if lo <= a)
-            return picked[g, first][:, a - first:b - first]
-
-        def mx_pass(acc, codes, scales, g, a, b):
+        def mx_pass(acc, tile_no, g, words, a, b, stop):
             nc.tensor.matmul_mx(
                 out=acc,
-                lhsT=codes[:, g * P:(g + 1) * P].bitcast(FP8X4),
-                lhsT_scale=scales[:, g * P:(g + 1) * P],
-                rhs=picked_words(g, a, b).bitcast(FP8X4),
+                lhsT=codes[tile_no][:, g * P:(g + 1) * P].bitcast(FP8X4),
+                lhsT_scale=scales[tile_no][:, g * P:(g + 1) * P],
+                rhs=words.bitcast(FP8X4),
                 rhs_scale=gs[ROWS * g:P, a:b],
                 start=(g == 0),
-                stop=(g == PASSES - 1),
+                stop=stop,
             )
 
-        h = keep.tile([P, S], F32, name="h0")
-        accs = [bank("b%d" % n, [P, b - a], "acc0_%d" % a) for n, (a, b) in enumerate(PIECES)]
+        h = {0: place([P, S], F32, "h0", None)}
+        accs0 = [bank(PRODUCT_BANKS[0][n], [P, b - a], "acc0_%d" % a) for n, (a, b) in enumerate(PIECES)]
         for g in range(PASSES):
-            for acc, (a, b) in zip(accs, PIECES):
-                mx_pass(acc[:], codes0, scales0, g, a, b)
-        for acc, (a, b) in zip(accs, PIECES):
+            for acc, (a, b) in zip(accs0, PIECES):
+                mx_pass(acc[:], 0, g, picked[g, a], a, b, g == PASSES - 1)
+        for acc, (a, b) in zip(accs0, PIECES):
             if a == 0:
-                nc.scalar.copy(h[:, a:b], acc[:])
+                nc.scalar.copy(h[0][:, a:b], acc[:])
             else:
-                nc.vector.tensor_copy(h[:, a:b], acc[:])
+                nc.vector.tensor_copy(h[0][:, a:b], acc[:])
 
-        codes1 = placed.tile([P, PASSES * P], U32, name="codes1", align_bytes=ALIGN, offset=CODES_AT[1])
-        scales1 = keep.tile([P, PASSES * P], U8, name="scales1", align_bytes=ALIGN)
-        quantise_half(1, 0, codes1, scales1, "second0")
+        accs = {}
 
-        def products(tile_no, codes, scales):
-            h_tile = placed.tile([P, S], F32, name="h%d" % tile_no, align_bytes=ALIGN, offset=H_AT[tile_no])
-            accs = [bank("b%d" % (H_BANKS * (tile_no % 2) + n), [P, b - a], "acc%d_%d" % (tile_no, a)) for n, (a, b) in enumerate(QUARTERS)]
-            for g in range(PASSES):
-                for acc, (a, b) in zip(accs, QUARTERS):
-                    mx_pass(acc[:], codes, scales, g, a, b)
-            for acc, (a, b) in zip(accs, QUARTERS):
-                nc.scalar.copy(h_tile[:, a:b], acc[:])
-            return h_tile
+        def first_pass(tile_no):
+            accs[tile_no] = [bank(number, [P, BANK], "acc%d_%d" % (tile_no, n)) for n, number in enumerate(PRODUCT_BANKS[tile_no])]
+            for n, acc in enumerate(accs[tile_no]):
+                mx_pass(acc[:], tile_no, 0, gw0[:, n * BANK:(n + 1) * BANK], n * BANK, (n + 1) * BANK, False)
 
-        result = keep.tile([P, V], F32, name="result")
+        def second_pass(tile_no):
+            for a, b in PIECES:
+                mx_pass(accs[tile_no][a // BANK][:, a % BANK:a % BANK + b - a], tile_no, 1, picked[1, a], a, b, b % BANK == 0)
 
-        def turn_back(run, b0, b1):
-            back = bank("b%d" % (H_BANKS + run + 1), [P, b1 - b0, 2, P], "back%d" % run)
-            for blk in range(b0, b1):
-                pairs = zb[blk][:].rearrange("v u p e -> v (u p e)").bitcast(F32)
-                for u in range(2):
-                    nc.tensor.transpose(back[:, blk - b0, u, :], pairs[:, u * P:(u + 1) * P], ident[:])
-            return back
+        def empty_banks(tile_no):
+            h[tile_no] = place([P, S], F32, "h%d" % tile_no, None)
+            for n, acc in enumerate(accs[tile_no]):
+                nc.scalar.copy(h[tile_no][:, n * BANK:(n + 1) * BANK], acc[:])
 
         def add_turned(total, term, start, stop):
-            nc.tensor.matmul(total, term, ident[:], start=start, stop=stop, is_transpose=True)
+            blocks = term.shape[1] // P
+            for n in range(blocks):
+                cols = slice(n * P, (n + 1) * P)
+                nc.tensor.matmul(total[:, cols], term[:, cols], ident[:], start=start and n == 0, stop=stop and n == blocks - 1, is_transpose=True)
 
+        def neighbour_term(term, tile_no, d, c0, c1):
+            nc.vector.tensor_tensor(term, h[tile_no][:].indirect(entries(neighbours[d], c0, c1)), gates[d][:, c0:c1], MULT)
+
+        def centre_term(tile_no):
+            centre = place([P, V], F32, "centre%d" % tile_no, None)
+            nc.scalar.activation(centre[:], h[tile_no][:].indirect(cen_t[:]), COPY, scale=-1.0)
+            return centre
+
+        zb = []
+
+        def round_sums(tile_no, total, b0, b1):
+            if not zb:
+                zb.append(place([P, BLOCKS * K_PASS], BF16, "zb", ZB_AT))
+            span = slice(P // PACK * tile_no, P // PACK * (tile_no + 1))
+            dst = zb[0][:].rearrange("v (b u p e) -> v b u p e", b=BLOCKS, u=2, e=2)[:, b0:b1, :, span, :]
+            nc.scalar.copy(dst, total.rearrange("v (b r u e) -> v b u r e", b=b1 - b0, u=2, e=2))
+
+        round_half(1, 0)
+        quantise_half(1, 0)
+        first_pass(1)
+        sums = {}
+        for tile_no in range(TILES - 1):
+            ahead = tile_no + 1
+            round_half(ahead, 1)
+            first_term = place([P, V], F32, "first_term%d" % tile_no, None)
+            neighbour_term(first_term[:], tile_no, 0, 0, V)
+            quantise_half(ahead, 1)
+            second_pass(ahead)
+            sums[tile_no] = bank(SUM_BANKS[tile_no], [P, V], "sum%d" % tile_no)
+            add_turned(sums[tile_no][:], first_term[:], True, False)
+            centre = centre_term(tile_no)
+            add_turned(sums[tile_no][:], centre[:], False, False)
+            if ahead + 1 < TILES:
+                round_half(ahead + 1, 0)
+            empty_banks(ahead)
+            later = place([P, D - 1, V], F32, "later%d" % tile_no, LATER_AT[tile_no])
+            for d in range(1, D):
+                neighbour_term(later[:, d - 1, :], tile_no, d, 0, V)
+                add_turned(sums[tile_no][:], later[:, d - 1, :], False, d == D - 1)
+            if ahead + 1 < TILES:
+                quantise_half(ahead + 1, 0)
+                first_pass(ahead + 1)
+
+        last = TILES - 1
+        round_sums(0, sums[0][:], 0, BLOCKS)
+        round_sums(1, sums[1][:], 0, BLOCKS)
+        centre = centre_term(last)
+        round_sums(2, sums[2][:], 0, BLOCKS)
+        terms = place([P, D, V], F32, "terms%d" % last, None)
         backs = []
-        codes2 = placed.tile([P, PASSES * P], U32, name="codes2", align_bytes=ALIGN, offset=CODES_AT[2])
-        codes3 = keep.tile([P, PASSES * P], U32, name="codes3", align_bytes=ALIGN)
-        scales3 = keep.tile([P, PASSES * P], U8, name="scales3", align_bytes=ALIGN)
-        scales2 = keep.tile([P, PASSES * P], U8, name="scales2", align_bytes=ALIGN)
-        for tile_no in range(TILES):
-            last = tile_no == TILES - 1
-            if tile_no == 1:
-                quantise_half(2, 0, codes2, scales2, "third0")
-                quantise_half(2, 1, codes2, scales2, None)
-                h_next = products(2, codes2, scales2)
-            if tile_no == 2:
-                quantise_half(3, 0, codes3, scales3, "fourth0")
-            if tile_no == 1:
-                four = placed.tile([P, D + 1, V], F32, name="terms1", align_bytes=ALIGN, offset=TERMS1_AT)
-                centre = four[:, D, :]
-            elif tile_no == 2:
-                centre = placed.tile([P, V], F32, name="centre2", align_bytes=ALIGN, offset=HALVES_AT[3][0])
-            else:
-                centre = keep.tile([P, V], F32, name="centre%d" % tile_no)
-            runs = RUNS if last else ((0, BLOCKS),)
-            c0, c1 = runs[0][0] * P, runs[0][1] * P
-            nc.vector.tensor_tensor(centre[:, c0:c1], h[:].indirect(entries(cen_t, c0, c1)), minus_one[:, c0:c1], MULT)
-            if tile_no == 0:
-                quantise_half(1, 1, codes1, scales1, "codes0")
-                h_next = products(1, codes1, scales1)
-                zb = [placed.tile([P, 2, P, 2], BF16, name="zb%d" % blk, align_bytes=ALIGN, offset=ZB_AT[blk]) for blk in range(BLOCKS)]
-                terms0 = placed.tile([P, D, V], F32, name="terms0", align_bytes=ALIGN, offset=RAW_AT[1])
-                terms = [terms0[:, d, :] for d in range(D)]
-            elif tile_no == 1:
-                terms = [four[:, d, :] for d in range(D)]
-            elif tile_no == 2:
-                quantise_half(3, 1, codes3, scales3, None)
-                h_next = products(3, codes3, scales3)
-                terms2 = placed.tile([P, D, V], F32, name="terms2", align_bytes=ALIGN, offset=HALVES_AT[3][1])
-                terms = [terms2[:, d, :] for d in range(D)]
-            else:
-                terms_n = keep.tile([P, D, V], F32, name="terms%d" % tile_no, align_bytes=ALIGN)
-                terms = [terms_n[:, d, :] for d in range(D)]
-            for run, (b0, b1) in enumerate(runs):
-                c0, c1 = b0 * P, b1 * P
-                if run > 0:
-                    nc.vector.tensor_tensor(centre[:, c0:c1], h[:].indirect(entries(cen_t, c0, c1)), minus_one[:, c0:c1], MULT)
-                sums = [bank("b%d" % (H_BANKS * ((tile_no + 1) % 2) + blk), [P, P], "sum%d_%d" % (tile_no, blk)) for blk in range(b0, b1)]
-                for blk in range(b0, b1):
-                    add_turned(sums[blk - b0][:], centre[:, blk * P:(blk + 1) * P], True, False)
-                for d in range(D):
-                    term = terms[d][:, c0:c1]
-                    if last and b1 == BLOCKS and d == D - 1:
-                        closing = placed.tile([P, c1 - c0], F32, name="closing", align_bytes=ALIGN, offset=ZB_AT[0])
-                        term = closing[:]
-                    nc.vector.tensor_tensor(term, h[:].indirect(entries(neighbours[d], c0, c1)), gates[d][:, c0:c1], MULT)
-                    for n in range(b1 - b0):
-                        add_turned(sums[n][:], term[:, n * P:(n + 1) * P], False, d == D - 1)
-                span = slice(P // PACK * tile_no, P // PACK * (tile_no + 1))
-                for blk in range(b0, b1):
-                    nc.scalar.activation(zb[blk][:, :, span, :], sums[blk - b0][:].rearrange("v (r u e) -> v u r e", u=2, e=2), COPY, scale=-1.0)
-                if last and run != 1:
-                    backs.extend(turn_back(r, RUNS[r][0], RUNS[r][1]) for r in range(len(backs), run + 1))
-            if not last:
-                h = h_next
+        for run, (b0, b1) in enumerate(RUNS):
+            c0, c1 = b0 * P, b1 * P
+            total = bank(RUN_SUM_BANKS[run], [P, c1 - c0], "sum%d_%d" % (last, run))
+            for d in range(D):
+                neighbour_term(terms[:, d, c0:c1], last, d, c0, c1)
+                if d == D - 1:
+                    add_turned(total[:], centre[:, c0:c1], False, False)
+                add_turned(total[:], terms[:, d, c0:c1], d == 0, d == D - 1)
+            round_sums(last, total[:], b0, b1)
+            back = bank(BACK_BANKS[run], [P, b1 - b0, 2, P], "back%d" % run)
+            pairs = zb[0][:].bitcast(F32)
+            for blk in range(b0, b1):
+                for u in range(2):
+                    at = (2 * blk + u) * P
+                    nc.tensor.transpose(back[:, blk - b0, u, :], pairs[:, at:at + P], ident[:])
+            backs.append(back)
 
+        result = place([P, V], F32, "result", None)
         for run, (b0, b1) in enumerate(RUNS):
             closing_run = run == len(RUNS) - 1
             width = (b1 - b0) * P
-            zq = keep.tile([P, width * PACK], BF16, name="zq%d" % run, align_bytes=ALIGN)
+            zq = place([P, width * PACK], BF16, "zq%d" % run, None)
             dst = zq[:].bitcast(F32).rearrange("p (b v u) -> p b v u", b=b1 - b0, u=2)
             src = backs[run][:].rearrange("p b u v -> p b v u")
             if closing_run:
                 nc.scalar.copy(dst, src)
             else:
                 nc.vector.tensor_copy(dst, src)
-            z_codes = keep.tile([P, width], U32, name="z_codes%d" % run, align_bytes=ALIGN)
-            z_scales = keep.tile([P, width], U8, name="z_scales%d" % run, align_bytes=ALIGN)
+            z_codes = place([P, width], U32, "z_codes%d" % run, None)
+            z_scales = place([P, width], U8, "z_scales%d" % run, None)
             nc.vector.quantize_mx(out=z_codes[:].bitcast(FP8X4), scales=z_scales[:], in_=zq[:])
-            product = bank("b%d" % run, [P, width], "product%d" % run)
+            product = bank(RESULT_BANKS[run], [P, width], "product%d" % run)
             nc.tensor.matmul_mx(
                 out=product[:],
                 lhsT=w2w[:].bitcast(FP4X4),
@@ -303,7 +302,7 @@ def tile_picked_lapl_none_p_kernel(tc, x_words, x_scales, w1, w2_words, w2_scale
             )
             cols = slice(b0 * P, b1 * P)
             if closing_run:
-                nc.vector.tensor_copy(result[:, cols], product[:])
+                nc.vector.tensor_scalar_mul(result[:, cols], product[:], -1.0)
             else:
-                nc.scalar.copy(result[:, cols], product[:])
+                nc.scalar.activation(result[:, cols], product[:], COPY, scale=-1.0)
             nc.sync.dma_start(out[:, cols], result[:, cols])

@@ -39,15 +39,16 @@ RAW1_AT = 36 * KIB
 GATES_AT = (34 * KIB, 10 * KIB, 12 * KIB)
 SECOND_AT = 26 * KIB
 W2_AT = 62 * KIB
-LATER_AT = (38 * KIB, 14 * KIB, 66 * KIB)
-CODES_AT = (44 * KIB, 47 * KIB, 50 * KIB, 53 * KIB)
-ROUNDED_AT = {(1, 1): CODES_AT[0], (2, 1): CODES_AT[1] - KIB // 2, (3, 0): CODES_AT[1] + KIB // 2, (3, 1): CODES_AT[2]}
-ZB_AT = CODES_AT[3]
+LATER_AT = (38 * KIB, 15 * KIB, 66 * KIB)
+CODES_AT = (44 * KIB, 47 * KIB, 51 * KIB, 56 * KIB)
+SCALES_AT = (None, None, 58 * KIB, None)
+ROUNDED_AT = {(1, 1): CODES_AT[0], (2, 0): RAW1_AT, (2, 1): CODES_AT[1], (3, 0): RAW_AT[2, 1], (3, 1): SCALES_AT[2]}
+ZB_AT = CODES_AT[2]
 PRODUCT_BANKS = ((0, 1, 2), (3, 1), (0, 2), (3, 1))
 SUM_BANKS = (4, 5, 6)
-RUN_SUM_BANKS = (7, 4, 7)
-BACK_BANKS = (0, 2, 3)
-RESULT_BANKS = (1, 5, 6)
+RUN_SUM_BANKS = (7, 0, 7)
+BACK_BANKS = (4, 5, 3)
+RESULT_BANKS = (1, 6, 7)
 
 
 def tile_picked_lapl_none_p_kernel(tc, x_words, x_scales, w1, w2_words, w2_scales, gate, offs, cen, pos1, pos2, pos3, out):
@@ -139,12 +140,17 @@ def tile_picked_lapl_none_p_kernel(tc, x_words, x_scales, w1, w2_words, w2_scale
 
         def round_half(tile_no, g):
             rounded[tile_no, g] = place([P, K_PASS], BF16, "rounded%d_%d" % (tile_no, g), ROUNDED_AT.get((tile_no, g)))
-            nc.scalar.copy(rounded[tile_no, g][:].rearrange("p (c t) -> p c t", t=PACK), raw[tile_no, g].rearrange("p t c -> p c t"))
+            dst = rounded[tile_no, g][:].rearrange("p (c t) -> p c t", t=PACK)
+            src = raw[tile_no, g].rearrange("p t c -> p c t")
+            if tile_no > 1 and g == 0:
+                nc.vector.tensor_copy(dst, src)
+            else:
+                nc.scalar.copy(dst, src)
 
         def quantise_half(tile_no, g):
             if g == 0:
                 codes[tile_no] = place([P, PASSES * P], U32, "codes%d" % tile_no, CODES_AT[tile_no])
-                scales[tile_no] = place([P, PASSES * P], U8, "scales%d" % tile_no, None)
+                scales[tile_no] = place([P, PASSES * P], U8, "scales%d" % tile_no, SCALES_AT[tile_no])
             cols = slice(g * P, (g + 1) * P)
             nc.vector.quantize_mx(out=codes[tile_no][:, cols].bitcast(FP8X4), scales=scales[tile_no][:, cols], in_=rounded[tile_no, g][:])
 
@@ -226,6 +232,9 @@ def tile_picked_lapl_none_p_kernel(tc, x_words, x_scales, w1, w2_words, w2_scale
             dst = zb[0][:].rearrange("v (b u p e) -> v b u p e", b=BLOCKS, u=2, e=2)[:, b0:b1, :, span, :]
             nc.scalar.copy(dst, total.rearrange("v (b r u e) -> v b u r e", b=b1 - b0, u=2, e=2))
 
+        def round_tile(tile_no):
+            round_sums(tile_no, sums[tile_no][:], 0, BLOCKS)
+
         round_half(1, 0)
         quantise_half(1, 0)
         first_pass(1)
@@ -241,11 +250,15 @@ def tile_picked_lapl_none_p_kernel(tc, x_words, x_scales, w1, w2_words, w2_scale
             add_turned(sums[tile_no][:], first_term[:], True, False)
             centre = centre_term(tile_no)
             add_turned(sums[tile_no][:], centre[:], False, False)
-            if ahead + 1 < TILES:
-                round_half(ahead + 1, 0)
+            if tile_no > 1:
+                round_tile(tile_no - 1)
             empty_banks(ahead)
+            if tile_no == 1:
+                round_tile(0)
             later = place([P, D - 1, V], F32, "later%d" % tile_no, LATER_AT[tile_no])
             for d in range(1, D):
+                if d == D - 1 and ahead + 1 < TILES:
+                    round_half(ahead + 1, 0)
                 neighbour_term(later[:, d - 1, :], tile_no, d, 0, V)
                 add_turned(sums[tile_no][:], later[:, d - 1, :], False, d == D - 1)
             if ahead + 1 < TILES:
@@ -253,21 +266,18 @@ def tile_picked_lapl_none_p_kernel(tc, x_words, x_scales, w1, w2_words, w2_scale
                 first_pass(ahead + 1)
 
         last = TILES - 1
-        round_sums(0, sums[0][:], 0, BLOCKS)
-        round_sums(1, sums[1][:], 0, BLOCKS)
         centre = centre_term(last)
-        round_sums(2, sums[2][:], 0, BLOCKS)
-        terms = place([P, D, V], F32, "terms%d" % last, None)
+        totals = {}
+
+        def open_run(run):
+            b0, b1 = RUNS[run]
+            totals[run] = bank(RUN_SUM_BANKS[run], [P, (b1 - b0) * P], "sum%d_%d" % (last, run))
+            add_turned(totals[run][:], centre[:, b0 * P:b1 * P], True, False)
+
         backs = []
-        for run, (b0, b1) in enumerate(RUNS):
-            c0, c1 = b0 * P, b1 * P
-            total = bank(RUN_SUM_BANKS[run], [P, c1 - c0], "sum%d_%d" % (last, run))
-            for d in range(D):
-                neighbour_term(terms[:, d, c0:c1], last, d, c0, c1)
-                if d == D - 1:
-                    add_turned(total[:], centre[:, c0:c1], False, False)
-                add_turned(total[:], terms[:, d, c0:c1], d == 0, d == D - 1)
-            round_sums(last, total[:], b0, b1)
+
+        def turn_back(run):
+            b0, b1 = RUNS[run]
             back = bank(BACK_BANKS[run], [P, b1 - b0, 2, P], "back%d" % run)
             pairs = zb[0][:].bitcast(F32)
             for blk in range(b0, b1):
@@ -275,6 +285,23 @@ def tile_picked_lapl_none_p_kernel(tc, x_words, x_scales, w1, w2_words, w2_scale
                     at = (2 * blk + u) * P
                     nc.tensor.transpose(back[:, blk - b0, u, :], pairs[:, at:at + P], ident[:])
             backs.append(back)
+
+        for run in range(len(RUNS) - 1):
+            open_run(run)
+        round_tile(last - 1)
+        terms = place([P, D, V], F32, "terms%d" % last, None)
+        for run, (b0, b1) in enumerate(RUNS):
+            c0, c1 = b0 * P, b1 * P
+            if run not in totals:
+                open_run(run)
+            for d in range(D):
+                neighbour_term(terms[:, d, c0:c1], last, d, c0, c1)
+                add_turned(totals[run][:], terms[:, d, c0:c1], False, d == D - 1)
+            round_sums(last, totals[run][:], b0, b1)
+            if run == 0:
+                turn_back(0)
+        for run in range(1, len(RUNS)):
+            turn_back(run)
 
         result = place([P, V], F32, "result", None)
         for run, (b0, b1) in enumerate(RUNS):

@@ -41,8 +41,7 @@ SECOND_AT = 26 * KIB
 W2_AT = 62 * KIB
 LATER_AT = (38 * KIB, 15 * KIB, 66 * KIB)
 CODES_AT = (44 * KIB, 47 * KIB, 51 * KIB, 56 * KIB)
-SCALES_AT = (None, None, 58 * KIB, None)
-ROUNDED_AT = {(1, 1): CODES_AT[0], (2, 0): RAW1_AT, (2, 1): CODES_AT[1], (3, 0): RAW_AT[2, 1], (3, 1): SCALES_AT[2]}
+ROUNDED_AT = {(1, 1): CODES_AT[0], (2, 1): CODES_AT[1] - KIB // 2, (3, 0): CODES_AT[1] + KIB // 2, (3, 1): CODES_AT[2]}
 ZB_AT = CODES_AT[2]
 PRODUCT_BANKS = ((0, 1, 2), (3, 1), (0, 2), (3, 1))
 SUM_BANKS = (4, 5, 6)
@@ -119,14 +118,14 @@ def tile_picked_lapl_none_p_kernel(tc, x_words, x_scales, w1, w2_words, w2_scale
             rows_q = gs[QUADRANT * q:QUADRANT * q + ROWS * PASSES, :]
             nc.sync.dma_start(rows_q.bitcast(I32), picked_rows[q:QUADRANT:QUADRANTS, :].bitcast(I32))
         raw1 = place([P, PASSES, PACK, P], F32, "raw1", RAW1_AT)
-        for g in range(PASSES):
-            load_w1(1, g, raw1[:, g, :, :])
+        load_w1(1, 0, raw1[:, 0, :, :])
         gates = [load_gate(0)]
+        load_w1(1, 1, raw1[:, 1, :, :])
         gw0 = place([P, S], U32, "gw0", None)
         nc.vector.tensor_copy(gw0[:], xw[0][:].bitcast(U32).indirect(offs_t[:]))
-        load_w1(2, 0)
-        gates.extend([load_gate(1), load_gate(2)])
-        load_w1(2, 1)
+        for g in range(PASSES):
+            gates.append(load_gate(1 + g))
+            load_w1(2, g)
         picked = {(0, a): gw0[:, a:b] for a, b in PIECES}
 
         def pick_second_pass(a, b, at):
@@ -142,15 +141,12 @@ def tile_picked_lapl_none_p_kernel(tc, x_words, x_scales, w1, w2_words, w2_scale
             rounded[tile_no, g] = place([P, K_PASS], BF16, "rounded%d_%d" % (tile_no, g), ROUNDED_AT.get((tile_no, g)))
             dst = rounded[tile_no, g][:].rearrange("p (c t) -> p c t", t=PACK)
             src = raw[tile_no, g].rearrange("p t c -> p c t")
-            if tile_no > 1 and g == 0:
-                nc.vector.tensor_copy(dst, src)
-            else:
-                nc.scalar.copy(dst, src)
+            nc.scalar.copy(dst, src)
 
         def quantise_half(tile_no, g):
             if g == 0:
                 codes[tile_no] = place([P, PASSES * P], U32, "codes%d" % tile_no, CODES_AT[tile_no])
-                scales[tile_no] = place([P, PASSES * P], U8, "scales%d" % tile_no, SCALES_AT[tile_no])
+                scales[tile_no] = place([P, PASSES * P], U8, "scales%d" % tile_no, None)
             cols = slice(g * P, (g + 1) * P)
             nc.vector.quantize_mx(out=codes[tile_no][:, cols].bitcast(FP8X4), scales=scales[tile_no][:, cols], in_=rounded[tile_no, g][:])
 
@@ -250,15 +246,13 @@ def tile_picked_lapl_none_p_kernel(tc, x_words, x_scales, w1, w2_words, w2_scale
             add_turned(sums[tile_no][:], first_term[:], True, False)
             centre = centre_term(tile_no)
             add_turned(sums[tile_no][:], centre[:], False, False)
-            if tile_no > 1:
-                round_tile(tile_no - 1)
-            empty_banks(ahead)
-            if tile_no == 1:
+            if ahead + 1 < TILES:
+                round_half(ahead + 1, 0)
+            else:
                 round_tile(0)
+            empty_banks(ahead)
             later = place([P, D - 1, V], F32, "later%d" % tile_no, LATER_AT[tile_no])
             for d in range(1, D):
-                if d == D - 1 and ahead + 1 < TILES:
-                    round_half(ahead + 1, 0)
                 neighbour_term(later[:, d - 1, :], tile_no, d, 0, V)
                 add_turned(sums[tile_no][:], later[:, d - 1, :], False, d == D - 1)
             if ahead + 1 < TILES:
@@ -288,7 +282,8 @@ def tile_picked_lapl_none_p_kernel(tc, x_words, x_scales, w1, w2_words, w2_scale
 
         for run in range(len(RUNS) - 1):
             open_run(run)
-        round_tile(last - 1)
+        for tile_no in range(1, last):
+            round_tile(tile_no)
         terms = place([P, D, V], F32, "terms%d" % last, None)
         for run, (b0, b1) in enumerate(RUNS):
             c0, c1 = b0 * P, b1 * P

@@ -139,8 +139,8 @@ def tile_picked_lapl_none_p_kernel(tc, x_words, x_scales, w1, w2_words, w2_scale
 
         def round_half(tile_no, g):
             rounded[tile_no, g] = place([P, K_PASS], BF16, "rounded%d_%d" % (tile_no, g), ROUNDED_AT.get((tile_no, g)))
-            dst = rounded[tile_no, g][:].rearrange("p (c t) -> p c t", t=PACK)
-            src = raw[tile_no, g].rearrange("p t c -> p c t")
+            dst = rounded[tile_no, g][:].rearrange("p (c i t) -> p c t i", i=PACK, t=PACK)
+            src = raw[tile_no, g].rearrange("p t (c i) -> p c t i", i=PACK)
             nc.scalar.copy(dst, src)
 
         def quantise_half(tile_no, g):

@@ -280,6 +280,12 @@ def tile_picked_lapl_none_p_kernel(tc, x_words, x_scales, w1, w2_words, w2_scale
                     nc.tensor.transpose(back[:, blk - b0, u, :], pairs[:, at:at + P], ident[:])
             backs.append(back)
 
+        def keep_clock(number):
+            idle = bank(number, [P, PASSES * P], "idle%d" % number)
+            for n in range(4):
+                nc.tensor.matmul_mx(out=idle[:], lhsT=codes[last][:, :P].bitcast(FP8X4), lhsT_scale=scales[last][:, :P], rhs=codes[last][:, :PASSES * P].bitcast(FP8X4), rhs_scale=scales[last][:], start=True, stop=True)
+
+        keep_clock(1)
         for run in range(len(RUNS) - 1):
             open_run(run)
         for tile_no in range(1, last):

@@ -42,7 +42,7 @@ W2_AT = 62 * KIB
 LATER_AT = (38 * KIB, 15 * KIB, 66 * KIB)
 CODES_AT = (44 * KIB, 47 * KIB, 51 * KIB, 56 * KIB)
 ROUNDED_AT = {(1, 1): CODES_AT[0], (2, 1): CODES_AT[1] - KIB // 2, (3, 0): CODES_AT[1] + KIB // 2, (3, 1): CODES_AT[2]}
-ZB_AT = CODES_AT[2]
+ZB_AT = RAW_AT[0, 1]
 PRODUCT_BANKS = ((0, 1, 2), (3, 1), (0, 2), (3, 1))
 SUM_BANKS = (4, 5, 6)
 RUN_SUM_BANKS = (7, 0, 7)
@@ -243,13 +243,11 @@ def tile_picked_lapl_none_p_kernel(tc, x_words, x_scales, w1, w2_words, w2_scale
             quantise_half(ahead, 1)
             second_pass(ahead)
             sums[tile_no] = bank(SUM_BANKS[tile_no], [P, V], "sum%d" % tile_no)
-            add_turned(sums[tile_no][:], first_term[:], True, False)
             centre = centre_term(tile_no)
-            add_turned(sums[tile_no][:], centre[:], False, False)
+            add_turned(sums[tile_no][:], centre[:], True, False)
+            add_turned(sums[tile_no][:], first_term[:], False, False)
             if ahead + 1 < TILES:
                 round_half(ahead + 1, 0)
-            else:
-                round_tile(0)
             empty_banks(ahead)
             later = place([P, D - 1, V], F32, "later%d" % tile_no, LATER_AT[tile_no])
             for d in range(1, D):
@@ -260,6 +258,7 @@ def tile_picked_lapl_none_p_kernel(tc, x_words, x_scales, w1, w2_words, w2_scale
                 first_pass(ahead + 1)
 
         last = TILES - 1
+        round_tile(0)
         centre = centre_term(last)
         totals = {}
 
@@ -285,7 +284,7 @@ def tile_picked_lapl_none_p_kernel(tc, x_words, x_scales, w1, w2_words, w2_scale
             for n in range(4):
                 nc.tensor.matmul_mx(out=idle[:], lhsT=codes[last][:, :P].bitcast(FP8X4), lhsT_scale=scales[last][:, :P], rhs=codes[last][:, :PASSES * P].bitcast(FP8X4), rhs_scale=scales[last][:], start=True, stop=True)
 
-        keep_clock(1)
+        keep_clock(SUM_BANKS[0])
         for run in range(len(RUNS) - 1):
             open_run(run)
         for tile_no in range(1, last):

@@ -32,6 +32,7 @@ ALIGN = 64
 PIECES = ((0, 512), (512, 768), (768, 1024))
 RUNS = ((0, 2), (2, 3), (3, 4))
 KIB = 1024
+SHARED = 256
 WORDS_AT = (8 * KIB, 60 * KIB)
 XS_AT = 35 * KIB
 RAW_AT = {(0, 0): 22 * KIB, (0, 1): 24 * KIB, (2, 0): 8 * KIB, (2, 1): 14 * KIB, (3, 0): 60 * KIB, (3, 1): 66 * KIB}
@@ -248,10 +249,16 @@ def tile_picked_lapl_none_p_kernel(tc, x_words, x_scales, w1, w2_words, w2_scale
             add_turned(sums[tile_no][:], first_term[:], False, False)
             if ahead + 1 < TILES:
                 round_half(ahead + 1, 0)
+            else:
+                plain = place([P, SHARED], F32, "plain", None)
+                nc.scalar.activation(plain[:], h[tile_no][:].indirect(entries(neighbours[D - 1], 0, SHARED)), COPY)
             empty_banks(ahead)
             later = place([P, D - 1, V], F32, "later%d" % tile_no, LATER_AT[tile_no])
             for d in range(1, D):
-                neighbour_term(later[:, d - 1, :], tile_no, d, 0, V)
+                shared = SHARED if tile_no == TILES - 2 and d == D - 1 else 0
+                if shared:
+                    nc.vector.tensor_tensor(later[:, d - 1, :shared], plain[:], gates[d][:, :shared], MULT)
+                neighbour_term(later[:, d - 1, shared:], tile_no, d, shared, V)
                 add_turned(sums[tile_no][:], later[:, d - 1, :], False, d == D - 1)
             if ahead + 1 < TILES:
                 quantise_half(ahead + 1, 0)

@@ -29,22 +29,22 @@ ROWS = 4
 PER_COLUMN = 16
 BANK = 512
 ALIGN = 64
-PIECES = ((0, 512), (512, 768), (768, 1024))
+PIECES = ((0, 512), (512, 768), (768, 896), (896, 1024))
 RUNS = ((0, 2), (2, 3), (3, 4))
 KIB = 1024
 SHARED = 256
 WORDS_AT = (8 * KIB, 60 * KIB)
 XS_AT = 35 * KIB
-RAW_AT = {(0, 0): 22 * KIB, (0, 1): 24 * KIB, (2, 0): 8 * KIB, (2, 1): 14 * KIB, (3, 0): 60 * KIB, (3, 1): 66 * KIB}
-RAW1_AT = 36 * KIB
-GATES_AT = (34 * KIB, 10 * KIB, 12 * KIB)
-SECOND_AT = 26 * KIB
+RAW_AT = {(0, 0): 22 * KIB, (0, 1): 24 * KIB, (1, 0): 36 * KIB, (1, 1): 6 * KIB + ALIGN, (2, 0): 14 * KIB + 2 * ALIGN, (2, 1): 22 * KIB, (3, 0): 60 * KIB, (3, 1): 66 * KIB}
+H_AT = {1: 15 * KIB}
+GATES_AT = (8 * KIB + 2 * ALIGN, 10 * KIB + 2 * ALIGN, 12 * KIB + 2 * ALIGN)
+SECOND_AT = (26 * KIB, RAW_AT[0, 1], RAW_AT[0, 1] + KIB, RAW_AT[0, 1] + KIB + KIB // 2)
 W2_AT = 62 * KIB
-LATER_AT = (38 * KIB, 15 * KIB, 66 * KIB)
+LATER_AT = (2 * KIB + 2 * ALIGN, 20 * KIB, 66 * KIB)
 CODES_AT = (44 * KIB, 47 * KIB, 51 * KIB, 56 * KIB)
-ROUNDED_AT = {(1, 1): CODES_AT[0], (2, 1): CODES_AT[1] - KIB // 2, (3, 0): CODES_AT[1] + KIB // 2, (3, 1): CODES_AT[2]}
+ROUNDED_AT = { (1, 1): CODES_AT[0], (2, 1): CODES_AT[1] - KIB // 2, (3, 0): CODES_AT[1] + KIB // 2, (3, 1): CODES_AT[2]}
 ZB_AT = RAW_AT[0, 1]
-PRODUCT_BANKS = ((0, 1, 2), (3, 1), (0, 2), (3, 1))
+PRODUCT_BANKS = ((0, 1, 2, 7), (3, 1), (0, 2), (3, 1))
 SUM_BANKS = (4, 5, 6)
 RUN_SUM_BANKS = (7, 0, 7)
 BACK_BANKS = (4, 5, 3)
@@ -94,9 +94,8 @@ def tile_picked_lapl_none_p_kernel(tc, x_words, x_scales, w1, w2_words, w2_scale
 
         raw = {}
 
-        def load_w1(tile_no, g, rows=None):
-            if rows is None:
-                rows = place([P, PACK, P], F32, "raw%d_%d" % (tile_no, g), RAW_AT[tile_no, g])[:]
+        def load_w1(tile_no, g):
+            rows = place([P, PACK, P], F32, "raw%d_%d" % (tile_no, g), RAW_AT[tile_no, g])[:]
             src = w1[g * K_PASS:(g + 1) * K_PASS, tile_no * P:(tile_no + 1) * P]
             nc.sync.dma_start(rows, src.rearrange("(p t) c -> p t c", t=PACK))
             raw[tile_no, g] = rows
@@ -105,28 +104,20 @@ def tile_picked_lapl_none_p_kernel(tc, x_words, x_scales, w1, w2_words, w2_scale
             rows_g = xs[ROWS * QUADRANTS * g:ROWS * QUADRANTS * (g + 1), :]
             nc.sync.dma_start(rows_g.bitcast(I32), x_scales[g].rearrange("(q j) n -> j q n", j=ROWS).bitcast(I32))
         offs_t = load_list(offs, "offs_t")
-        xw = [load_words(0)]
-        load_w1(0, 0)
-        cen_t = load_list(cen, "cen_t")
-        neighbours = [load_list(pos1, "pos1_t")]
-        xw.append(load_words(1))
-        load_w1(0, 1)
-        neighbours.extend([load_list(pos2, "pos2_t"), load_list(pos3, "pos3_t")])
+        xw = []
+        for g in range(PASSES):
+            xw.append(load_words(g))
+            load_w1(0, g)
 
         picked_rows = place([P, S], U8, "picked_rows", None)
         nc.vector.tensor_copy(picked_rows[:], xs[:].indirect(offs_t[:]))
         for q in range(QUADRANTS):
             rows_q = gs[QUADRANT * q:QUADRANT * q + ROWS * PASSES, :]
             nc.sync.dma_start(rows_q.bitcast(I32), picked_rows[q:QUADRANT:QUADRANTS, :].bitcast(I32))
-        raw1 = place([P, PASSES, PACK, P], F32, "raw1", RAW1_AT)
-        load_w1(1, 0, raw1[:, 0, :, :])
-        gates = [load_gate(0)]
-        load_w1(1, 1, raw1[:, 1, :, :])
+        load_w1(1, 0)
+        neighbours = [load_list(pos1, "pos1_t")]
         gw0 = place([P, S], U32, "gw0", None)
         nc.vector.tensor_copy(gw0[:], xw[0][:].bitcast(U32).indirect(offs_t[:]))
-        for g in range(PASSES):
-            gates.append(load_gate(1 + g))
-            load_w1(2, g)
         picked = {(0, a): gw0[:, a:b] for a, b in PIECES}
 
         def pick_second_pass(a, b, at):
@@ -152,12 +143,19 @@ def tile_picked_lapl_none_p_kernel(tc, x_words, x_scales, w1, w2_words, w2_scale
             nc.vector.quantize_mx(out=codes[tile_no][:, cols].bitcast(FP8X4), scales=scales[tile_no][:, cols], in_=rounded[tile_no, g][:])
 
         round_half(0, 0)
+        gates = [load_gate(0)]
+        load_w1(1, 1)
+        cen_t = load_list(cen, "cen_t")
+        for g, later_list in enumerate((pos2, pos3)):
+            neighbours.append(load_list(later_list, "pos%d_t" % (2 + g)))
+            gates.append(load_gate(1 + g))
+            load_w1(2, g)
         quantise_half(0, 0)
-        for a, b in PIECES[:-1]:
-            pick_second_pass(a, b, SECOND_AT + PACK * a)
-        round_half(0, 1)
-        quantise_half(0, 1)
-        pick_second_pass(PIECES[-1][0], PIECES[-1][1], RAW_AT[0, 1])
+        for (a, b), at in zip(PIECES, SECOND_AT):
+            pick_second_pass(a, b, at)
+            if a == 0:
+                round_half(0, 1)
+                quantise_half(0, 1)
         for g in range(PASSES):
             load_w1(3, g)
         w2w = place([P, 2 * N], U8, "w2w", W2_AT)
@@ -185,7 +183,7 @@ def tile_picked_lapl_none_p_kernel(tc, x_words, x_scales, w1, w2_words, w2_scale
             for acc, (a, b) in zip(accs0, PIECES):
                 mx_pass(acc[:], 0, g, picked[g, a], a, b, g == PASSES - 1)
         for acc, (a, b) in zip(accs0, PIECES):
-            if a == 0:
+            if a == 0 or b == S:
                 nc.scalar.copy(h[0][:, a:b], acc[:])
             else:
                 nc.vector.tensor_copy(h[0][:, a:b], acc[:])
@@ -202,7 +200,7 @@ def tile_picked_lapl_none_p_kernel(tc, x_words, x_scales, w1, w2_words, w2_scale
                 mx_pass(accs[tile_no][a // BANK][:, a % BANK:a % BANK + b - a], tile_no, 1, picked[1, a], a, b, b % BANK == 0)
 
         def empty_banks(tile_no):
-            h[tile_no] = place([P, S], F32, "h%d" % tile_no, None)
+            h[tile_no] = place([P, S], F32, "h%d" % tile_no, H_AT.get(tile_no))
             for n, acc in enumerate(accs[tile_no]):
                 nc.scalar.copy(h[tile_no][:, n * BANK:(n + 1) * BANK], acc[:])
 

@@ -35,12 +35,12 @@ KIB = 1024
 SHARED = 256
 WORDS_AT = (8 * KIB, 60 * KIB)
 XS_AT = 35 * KIB
-RAW_AT = {(0, 0): 22 * KIB, (0, 1): 24 * KIB, (1, 0): 36 * KIB, (1, 1): 6 * KIB + ALIGN, (2, 0): 14 * KIB + 2 * ALIGN, (2, 1): 22 * KIB, (3, 0): 60 * KIB, (3, 1): 66 * KIB}
+RAW_AT = {(0, 0): 22 * KIB, (0, 1): 24 * KIB, (1, 0): 34 * KIB - ALIGN, (1, 1): 36 * KIB - ALIGN, (2, 0): 14 * KIB + 2 * ALIGN, (2, 1): 22 * KIB, (3, 0): 60 * KIB, (3, 1): 66 * KIB}
 H_AT = {1: 15 * KIB}
 GATES_AT = (8 * KIB + 2 * ALIGN, 10 * KIB + 2 * ALIGN, 12 * KIB + 2 * ALIGN)
 SECOND_AT = (26 * KIB, RAW_AT[0, 1], RAW_AT[0, 1] + KIB, RAW_AT[0, 1] + KIB + KIB // 2)
 W2_AT = 62 * KIB
-LATER_AT = (2 * KIB + 2 * ALIGN, 20 * KIB, 66 * KIB)
+LATER_AT = (RAW_AT[1, 1], 20 * KIB, 66 * KIB)
 CODES_AT = (44 * KIB, 47 * KIB, 51 * KIB, 56 * KIB)
 ROUNDED_AT = { (1, 1): CODES_AT[0], (2, 1): CODES_AT[1] - KIB // 2, (3, 0): CODES_AT[1] + KIB // 2, (3, 1): CODES_AT[2]}
 ZB_AT = RAW_AT[0, 1]
@@ -72,6 +72,8 @@ def tile_picked_lapl_none_p_kernel(tc, x_words, x_scales, w1, w2_words, w2_scale
         xs = place([P, T], U8, "xs", XS_AT)
         nc.vector.memset(xs[QUADRANT:2 * QUADRANT, :].bitcast(I32), 0)
         nc.vector.memset(xs[2 * QUADRANT:P, :].bitcast(I32), 0)
+        w2s = place([P, N], U8, "w2s", None)
+        nc.vector.memset(w2s[:].bitcast(I32), 0)
         gs = place([P, S], U8, "gs", None)
         nc.gpsimd.memset(gs[:].bitcast(I32), 0)
         ident = place([P, P], F32, "ident", None)
@@ -114,7 +116,8 @@ def tile_picked_lapl_none_p_kernel(tc, x_words, x_scales, w1, w2_words, w2_scale
         for q in range(QUADRANTS):
             rows_q = gs[QUADRANT * q:QUADRANT * q + ROWS * PASSES, :]
             nc.sync.dma_start(rows_q.bitcast(I32), picked_rows[q:QUADRANT:QUADRANTS, :].bitcast(I32))
-        load_w1(1, 0)
+        for g in range(PASSES):
+            load_w1(1, g)
         neighbours = [load_list(pos1, "pos1_t")]
         gw0 = place([P, S], U32, "gw0", None)
         nc.vector.tensor_copy(gw0[:], xw[0][:].bitcast(U32).indirect(offs_t[:]))
@@ -144,7 +147,6 @@ def tile_picked_lapl_none_p_kernel(tc, x_words, x_scales, w1, w2_words, w2_scale
 
         round_half(0, 0)
         gates = [load_gate(0)]
-        load_w1(1, 1)
         cen_t = load_list(cen, "cen_t")
         for g, later_list in enumerate((pos2, pos3)):
             neighbours.append(load_list(later_list, "pos%d_t" % (2 + g)))
@@ -160,8 +162,6 @@ def tile_picked_lapl_none_p_kernel(tc, x_words, x_scales, w1, w2_words, w2_scale
             load_w1(3, g)
         w2w = place([P, 2 * N], U8, "w2w", W2_AT)
         nc.sync.dma_start(w2w[:].bitcast(I32), w2_words[0].bitcast(I32))
-        w2s = place([P, N], U8, "w2s", W2_AT + 2 * N)
-        nc.vector.memset(w2s[:].bitcast(I32), 0)
         for q in range(QUADRANTS):
             rows_q = w2s[QUADRANT * q:QUADRANT * q + ROWS, :]
             nc.sync.dma_start(rows_q.bitcast(I32), w2_scales[0, ROWS * q:ROWS * (q + 1), :].bitcast(I32))

from contextlib import ExitStack

import concourse.mybir as mybir
from concourse.masks import make_identity

K, T, S, D, V, H, N = 1024, 2048, 1024, 3, 512, 512, 128
FLOPS = 2 * K * H * S + 2 * H * N * V

F32 = mybir.dt.float32
BF16 = mybir.dt.bfloat16
I32 = mybir.dt.int32
U32 = mybir.dt.uint32
U16 = mybir.dt.uint16
U8 = mybir.dt.uint8
FP8X4 = mybir.dt.float8_e4m3fn_x4
FP4X4 = mybir.dt.float4_e2m1fn_x4
MULT = mybir.AluOpType.mult
COPY = mybir.ActivationFunctionType.Copy

P = 128
PACK = 4
K_PASS = P * PACK
PASSES = K // K_PASS
TILES = H // P
BLOCKS = V // P
QUADRANT = 32
QUADRANTS = P // QUADRANT
ROWS = 4
PER_COLUMN = 16
BANK = 512
ALIGN = 64
PIECES = ((0, 512), (512, 768), (768, 896), (896, 1024))
RUNS = ((0, 2), (2, 3), (3, 4))
KIB = 1024
SHARED = 256
WORDS_AT = (8 * KIB, 60 * KIB)
XS_AT = 35 * KIB
RAW_AT = {(0, 0): 22 * KIB, (0, 1): 24 * KIB, (1, 0): 34 * KIB - ALIGN, (1, 1): 36 * KIB - ALIGN, (2, 0): 14 * KIB + 2 * ALIGN, (2, 1): 22 * KIB, (3, 0): 60 * KIB, (3, 1): 66 * KIB}
H_AT = {1: 15 * KIB}
GATES_AT = (8 * KIB + 2 * ALIGN, 10 * KIB + 2 * ALIGN, 12 * KIB + 2 * ALIGN)
SECOND_AT = (26 * KIB, RAW_AT[0, 1], RAW_AT[0, 1] + KIB, RAW_AT[0, 1] + KIB + KIB // 2)
W2_AT = 62 * KIB
LATER_AT = (RAW_AT[1, 1], 20 * KIB, 66 * KIB)
CODES_AT = (44 * KIB, 47 * KIB, 51 * KIB, 56 * KIB)
ROUNDED_AT = { (1, 1): CODES_AT[0], (2, 1): CODES_AT[1] - KIB // 2, (3, 0): CODES_AT[1] + KIB // 2, (3, 1): CODES_AT[2]}
ZB_AT = RAW_AT[0, 1]
PRODUCT_BANKS = ((0, 1, 2, 7), (3, 1), (0, 2), (3, 1))
SUM_BANKS = (4, 5, 6)
RUN_SUM_BANKS = (7, 0, 7)
BACK_BANKS = (4, 5, 3)
RESULT_BANKS = (1, 6, 7)


def tile_picked_lapl_none_p_kernel(tc, x_words, x_scales, w1, w2_words, w2_scales, gate, offs, cen, pos1, pos2, pos3, out):
    nc = tc.nc
    with ExitStack() as ctx:
        keep = ctx.enter_context(tc.tile_pool(name="keep", bufs=1))
        psum = ctx.enter_context(tc.psum_pool(name="psum", bufs=1))
        placed = ctx.enter_context(tc.tile_pool(name="placed", bufs=1))

        def bank(number, shape, name):
            return psum.tile(shape, F32, name=name, tag="b%d" % number)

        def place(shape, dtype, name, at):
            if at is None:
                return keep.tile(shape, dtype, name=name, align_bytes=ALIGN)
            return placed.tile(shape, dtype, name=name, align_bytes=ALIGN, offset=at)

        def entries(list_tile, a, b):
            return list_tile[:, a // PER_COLUMN:b // PER_COLUMN]

        xs = place([P, T], U8, "xs", XS_AT)
        nc.vector.memset(xs[QUADRANT:2 * QUADRANT, :].bitcast(I32), 0)
        nc.vector.memset(xs[2 * QUADRANT:P, :].bitcast(I32), 0)
        w2s = place([P, N], U8, "w2s", None)
        nc.vector.memset(w2s[:].bitcast(I32), 0)
        gs = place([P, S], U8, "gs", None)
        nc.gpsimd.memset(gs[:].bitcast(I32), 0)
        ident = place([P, P], F32, "ident", None)
        make_identity(nc, ident[:])

        def load_list(src, name):
            list_tile = keep.tile(list(src.shape), U16, name=name)
            nc.sync.dma_start(list_tile[:], src)
            return list_tile

        def load_words(g):
            table = place([P, T], I32, "xw%d" % g, WORDS_AT[g])
            nc.sync.dma_start(table[:], x_words[g].rearrange("p n t -> p (n t)").bitcast(I32))
            return table

        def load_gate(d):
            weights = place([P, V], F32, "gate%d" % d, GATES_AT[d])
            nc.sync.dma_start(weights[:], gate[d])
            return weights

        raw = {}

        def load_w1(tile_no, g):
            rows = place([P, PACK, P], F32, "raw%d_%d" % (tile_no, g), RAW_AT[tile_no, g])[:]
            src = w1[g * K_PASS:(g + 1) * K_PASS, tile_no * P:(tile_no + 1) * P]
            nc.sync.dma_start(rows, src.rearrange("(p t) c -> p t c", t=PACK))
            raw[tile_no, g] = rows

        for g in range(PASSES):
            rows_g = xs[ROWS * QUADRANTS * g:ROWS * QUADRANTS * (g + 1), :]
            nc.sync.dma_start(rows_g.bitcast(I32), x_scales[g].rearrange("(q j) n -> j q n", j=ROWS).bitcast(I32))
        offs_t = load_list(offs, "offs_t")
        xw = []
        for g in range(PASSES):
            xw.append(load_words(g))
            load_w1(0, g)

        picked_rows = place([P, S], U8, "picked_rows", None)
        nc.vector.tensor_copy(picked_rows[:], xs[:].indirect(offs_t[:]))
        for q in range(QUADRANTS):
            rows_q = gs[QUADRANT * q:QUADRANT * q + ROWS * PASSES, :]
            nc.sync.dma_start(rows_q.bitcast(I32), picked_rows[q:QUADRANT:QUADRANTS, :].bitcast(I32))
        for g in range(PASSES):
            load_w1(1, g)
        neighbours = [load_list(pos1, "pos1_t")]
        gw0 = place([P, S], U32, "gw0", None)
        nc.vector.tensor_copy(gw0[:], xw[0][:].bitcast(U32).indirect(offs_t[:]))
        picked = {(0, a): gw0[:, a:b] for a, b in PIECES}

        def pick_second_pass(a, b, at):
            words = place([P, b - a], U32, "gw1_%d" % a, at)
            nc.vector.tensor_copy(words[:], xw[1][:].bitcast(U32).indirect(entries(offs_t, a, b)))
            picked[1, a] = words[:]

        codes = {}
        scales = {}
        rounded = {}

        def round_half(tile_no, g):
            rounded[tile_no, g] = place([P, K_PASS], BF16, "rounded%d_%d" % (tile_no, g), ROUNDED_AT.get((tile_no, g)))
            dst = rounded[tile_no, g][:].rearrange("p (c i t) -> p c t i", i=PACK, t=PACK)
            src = raw[tile_no, g].rearrange("p t (c i) -> p c t i", i=PACK)
            nc.scalar.copy(dst, src)

        def quantise_half(tile_no, g):
            if g == 0:
                codes[tile_no] = place([P, PASSES * P], U32, "codes%d" % tile_no, CODES_AT[tile_no])
                scales[tile_no] = place([P, PASSES * P], U8, "scales%d" % tile_no, None)
            cols = slice(g * P, (g + 1) * P)
            nc.vector.quantize_mx(out=codes[tile_no][:, cols].bitcast(FP8X4), scales=scales[tile_no][:, cols], in_=rounded[tile_no, g][:])

        round_half(0, 0)
        gates = [load_gate(0)]
        cen_t = load_list(cen, "cen_t")
        for g, later_list in enumerate((pos2, pos3)):
            neighbours.append(load_list(later_list, "pos%d_t" % (2 + g)))
            gates.append(load_gate(1 + g))
            load_w1(2, g)
        quantise_half(0, 0)
        for (a, b), at in zip(PIECES, SECOND_AT):
            pick_second_pass(a, b, at)
            if a == 0:
                round_half(0, 1)
                quantise_half(0, 1)
        for g in range(PASSES):
            load_w1(3, g)
        w2w = place([P, 2 * N], U8, "w2w", W2_AT)
        nc.sync.dma_start(w2w[:].bitcast(I32), w2_words[0].bitcast(I32))
        for q in range(QUADRANTS):
            rows_q = w2s[QUADRANT * q:QUADRANT * q + ROWS, :]
            nc.sync.dma_start(rows_q.bitcast(I32), w2_scales[0, ROWS * q:ROWS * (q + 1), :].bitcast(I32))

        def mx_pass(acc, tile_no, g, words, a, b, stop):
            nc.tensor.matmul_mx(
                out=acc,
                lhsT=codes[tile_no][:, g * P:(g + 1) * P].bitcast(FP8X4),
                lhsT_scale=scales[tile_no][:, g * P:(g + 1) * P],
                rhs=words.bitcast(FP8X4),
                rhs_scale=gs[ROWS * g:P, a:b],
                start=(g == 0),
                stop=stop,
            )

        h = {0: place([P, S], F32, "h0", None)}
        accs0 = [bank(PRODUCT_BANKS[0][n], [P, b - a], "acc0_%d" % a) for n, (a, b) in enumerate(PIECES)]
        for g in range(PASSES):
            for acc, (a, b) in zip(accs0, PIECES):
                mx_pass(acc[:], 0, g, picked[g, a], a, b, g == PASSES - 1)
        for acc, (a, b) in zip(accs0, PIECES):
            if a == 0 or b == S:
                nc.scalar.copy(h[0][:, a:b], acc[:])
            else:
                nc.vector.tensor_copy(h[0][:, a:b], acc[:])

        accs = {}

        def first_pass(tile_no):
            accs[tile_no] = [bank(number, [P, BANK], "acc%d_%d" % (tile_no, n)) for n, number in enumerate(PRODUCT_BANKS[tile_no])]
            for n, acc in enumerate(accs[tile_no]):
                mx_pass(acc[:], tile_no, 0, gw0[:, n * BANK:(n + 1) * BANK], n * BANK, (n + 1) * BANK, False)

        def second_pass(tile_no):
            for a, b in PIECES:
                mx_pass(accs[tile_no][a // BANK][:, a % BANK:a % BANK + b - a], tile_no, 1, picked[1, a], a, b, b % BANK == 0)

        def empty_banks(tile_no):
            h[tile_no] = place([P, S], F32, "h%d" % tile_no, H_AT.get(tile_no))
            for n, acc in enumerate(accs[tile_no]):
                nc.scalar.copy(h[tile_no][:, n * BANK:(n + 1) * BANK], acc[:])

        def add_turned(total, term, start, stop):
            blocks = term.shape[1] // P
            for n in range(blocks):
                cols = slice(n * P, (n + 1) * P)
                nc.tensor.matmul(total[:, cols], term[:, cols], ident[:], start=start and n == 0, stop=stop and n == blocks - 1, is_transpose=True)

        def neighbour_term(term, tile_no, d, c0, c1):
            nc.vector.tensor_tensor(term, h[tile_no][:].indirect(entries(neighbours[d], c0, c1)), gates[d][:, c0:c1], MULT)

        def centre_term(tile_no):
            centre = place([P, V], F32, "centre%d" % tile_no, None)
            nc.scalar.activation(centre[:], h[tile_no][:].indirect(cen_t[:]), COPY, scale=-1.0)
            return centre

        zb = []

        def round_sums(tile_no, total, b0, b1):
            if not zb:
                zb.append(place([P, BLOCKS * K_PASS], BF16, "zb", ZB_AT))
            span = slice(P // PACK * tile_no, P // PACK * (tile_no + 1))
            dst = zb[0][:].rearrange("v (b u p e) -> v b u p e", b=BLOCKS, u=2, e=2)[:, b0:b1, :, span, :]
            nc.scalar.copy(dst, total.rearrange("v (b r u e) -> v b u r e", b=b1 - b0, u=2, e=2))

        def round_tile(tile_no):
            round_sums(tile_no, sums[tile_no][:], 0, BLOCKS)

        round_half(1, 0)
        quantise_half(1, 0)
        first_pass(1)
        sums = {}
        for tile_no in range(TILES - 1):
            ahead = tile_no + 1
            round_half(ahead, 1)
            first_term = place([P, V], F32, "first_term%d" % tile_no, None)
            neighbour_term(first_term[:], tile_no, 0, 0, V)
            quantise_half(ahead, 1)
            second_pass(ahead)
            sums[tile_no] = bank(SUM_BANKS[tile_no], [P, V], "sum%d" % tile_no)
            centre = centre_term(tile_no)
            add_turned(sums[tile_no][:], centre[:], True, False)
            add_turned(sums[tile_no][:], first_term[:], False, False)
            if ahead + 1 < TILES:
                round_half(ahead + 1, 0)
            else:
                plain = place([P, SHARED], F32, "plain", None)
                nc.scalar.activation(plain[:], h[tile_no][:].indirect(entries(neighbours[D - 1], 0, SHARED)), COPY)
            empty_banks(ahead)
            later = place([P, D - 1, V], F32, "later%d" % tile_no, LATER_AT[tile_no])
            for d in range(1, D):
                shared = SHARED if tile_no == TILES - 2 and d == D - 1 else 0
                if shared:
                    nc.vector.tensor_tensor(later[:, d - 1, :shared], plain[:], gates[d][:, :shared], MULT)
                neighbour_term(later[:, d - 1, shared:], tile_no, d, shared, V)
                add_turned(sums[tile_no][:], later[:, d - 1, :], False, d == D - 1)
            if ahead + 1 < TILES:
                quantise_half(ahead + 1, 0)
                first_pass(ahead + 1)

        last = TILES - 1
        round_tile(0)
        centre = centre_term(last)
        totals = {}

        def open_run(run):
            b0, b1 = RUNS[run]
            totals[run] = bank(RUN_SUM_BANKS[run], [P, (b1 - b0) * P], "sum%d_%d" % (last, run))
            add_turned(totals[run][:], centre[:, b0 * P:b1 * P], True, False)

        backs = []

        def turn_back(run):
            b0, b1 = RUNS[run]
            back = bank(BACK_BANKS[run], [P, b1 - b0, 2, P], "back%d" % run)
            pairs = zb[0][:].bitcast(F32)
            for blk in range(b0, b1):
                for u in range(2):
                    at = (2 * blk + u) * P
                    nc.tensor.transpose(back[:, blk - b0, u, :], pairs[:, at:at + P], ident[:])
            backs.append(back)

        def keep_clock(number):
            idle = bank(number, [P, PASSES * P], "idle%d" % number)
            for n in range(4):
                nc.tensor.matmul_mx(out=idle[:], lhsT=codes[last][:, :P].bitcast(FP8X4), lhsT_scale=scales[last][:, :P], rhs=codes[last][:, :PASSES * P].bitcast(FP8X4), rhs_scale=scales[last][:], start=True, stop=True)

        keep_clock(SUM_BANKS[0])
        for run in range(len(RUNS) - 1):
            open_run(run)
        for tile_no in range(1, last):
            round_tile(tile_no)
        terms = place([P, D, V], F32, "terms%d" % last, None)
        for run, (b0, b1) in enumerate(RUNS):
            c0, c1 = b0 * P, b1 * P
            if run not in totals:
                open_run(run)
            for d in range(D):
                neighbour_term(terms[:, d, c0:c1], last, d, c0, c1)
                add_turned(totals[run][:], terms[:, d, c0:c1], False, d == D - 1)
            round_sums(last, totals[run][:], b0, b1)
            if run == 0:
                turn_back(0)
        for run in range(1, len(RUNS)):
            turn_back(run)

        result = place([P, V], F32, "result", None)
        for run, (b0, b1) in enumerate(RUNS):
            closing_run = run == len(RUNS) - 1
            width = (b1 - b0) * P
            zq = place([P, width * PACK], BF16, "zq%d" % run, None)
            dst = zq[:].bitcast(F32).rearrange("p (b v u) -> p b v u", b=b1 - b0, u=2)
            src = backs[run][:].rearrange("p b u v -> p b v u")
            if closing_run:
                nc.scalar.copy(dst, src)
            else:
                nc.vector.tensor_copy(dst, src)
            z_codes = place([P, width], U32, "z_codes%d" % run, None)
            z_scales = place([P, width], U8, "z_scales%d" % run, None)
            nc.vector.quantize_mx(out=z_codes[:].bitcast(FP8X4), scales=z_scales[:], in_=zq[:])
            product = bank(RESULT_BANKS[run], [P, width], "product%d" % run)
            nc.tensor.matmul_mx(
                out=product[:],
                lhsT=w2w[:].bitcast(FP4X4),
                lhsT_scale=w2s[:],
                rhs=z_codes[:].bitcast(FP8X4),
                rhs_scale=z_scales[:],
                start=True,
                stop=True,
            )
            cols = slice(b0 * P, b1 * P)
            if closing_run:
                nc.vector.tensor_scalar_mul(result[:, cols], product[:], -1.0)
            else:
                nc.scalar.activation(result[:, cols], product[:], COPY, scale=-1.0)
            nc.sync.dma_start(out[:, cols], result[:, cols])
